import numpy as np
import ml_dtypes


def mxq(x, axis, fmt="e4m3"):
    dtype, down = {"e4m3": (ml_dtypes.float8_e4m3fn, 7), "e5m2": (ml_dtypes.float8_e5m2, 14)}[fmt]
    v = np.moveaxis(np.asarray(x, np.float32).astype(ml_dtypes.bfloat16).astype(np.float64), axis, -1)
    blocks = v.reshape(v.shape[:-1] + (-1, 32))
    amax = np.abs(blocks).max(-1, keepdims=True)
    byte = np.maximum(np.where(amax > 0, np.frexp(amax)[1] - 1 + 127, 0) - down, 1)
    scale = np.exp2(byte - 127.0)
    codes = (blocks / scale).astype(np.float32).astype(dtype).astype(np.float64)
    return np.moveaxis((codes * scale).reshape(v.shape), -1, axis)


WIDE = False


def mx_kscale(k):
    if not WIDE:
        return np.ones(k)
    levels = np.array([10, -10, 5, -5, 0])
    if k % 512:
        return np.exp2(np.random.permutation(np.resize(levels, k // 32))).repeat(32)
    a = np.empty((k // 512, 16))
    for p in range(k // 512):
        a[p, :8] = np.random.permutation(np.resize(levels, 8))
        for g in range(8):
            far = levels[np.abs(levels - a[p, g]) >= 10]
            a[p, g + 8] = far[np.random.randint(len(far))]
    return np.exp2(a.ravel()).repeat(32)


def f64(x):
    return np.asarray(x).astype(np.float64)


def striped(idx):
    return np.tile(idx.reshape(-1, 16).T, (8, 1)).astype(np.uint16)


def unstriped(offs):
    return offs[:16].T.reshape(-1).astype(np.int64)


E2M1 = np.array([0.0, 0.5, 1.0, 1.5, 2.0, 3.0, 4.0, 6.0, -0.0, -0.5, -1.0, -1.5, -2.0, -3.0, -4.0, -6.0])


def pack_fp4(w):
    k, n = w.shape
    w = f64(np.asarray(w, np.float32).astype(ml_dtypes.bfloat16)).reshape(k // 32, 32, n)
    amax = np.abs(w).max(1)
    mant, ex = np.frexp(amax / 6.0)
    byte = np.clip(np.where(amax > 0, np.where(mant > 0.5, ex, ex - 1) + 127, 1), 1, 254)
    scaled = (w * np.exp2(127.0 - byte)[:, None, :]).reshape(k, n).astype(np.float32)
    c = np.ascontiguousarray(scaled.reshape(k // 512, 128, 4, n).transpose(0, 1, 3, 2)).astype(ml_dtypes.float4_e2m1fn).view(np.uint8) & 0xF
    words = (c[..., 0::2] | (c[..., 1::2] << 4)).reshape(k // 512, 128, 2 * n)
    return np.ascontiguousarray(words), np.ascontiguousarray(byte.astype(np.uint8).reshape(k // 512, 16, n))


def unpack_fp4(words, scales):
    g, _, n = scales.shape
    words = np.ascontiguousarray(words).reshape(g, 128, n, 2)
    nib = np.empty((g, 128, n, 4), np.uint8)
    nib[..., 0::2] = words & 0xF
    nib[..., 1::2] = words >> 4
    vals = E2M1[nib] * np.repeat(np.exp2(scales.astype(np.float64) - 127.0), 8, axis=1)[..., None]
    return vals.transpose(0, 1, 3, 2).reshape(g * 512, n)


K, T, S, N = 1024, 1024, 512, 256
P = 2 ** 7


def setup_inputs():
    n = np.random.standard_normal
    s = mx_kscale(K)[:, None]
    packed_w1 = pack_fp4(n((K, N)) / np.sqrt(K) / s)
    return {
        "xT": (n((K, T)) * s).astype(np.float32),
        "tscale": np.tile(np.random.uniform(0.25, 2.0, T), (P, 1)).astype(np.float32),
        "cscale": np.random.uniform(0.5, 1.5, (N, 1)).astype(np.float32),
        "w1_words": packed_w1[0],
        "w1_scales": packed_w1[1],
        "offs": striped(np.random.permutation(T)[:S]),
    }


def reference(xT, tscale, cscale, w1_words, w1_scales, offs):
    xq = mxq(f64(xT)[:, unstriped(offs)], 0, "e4m3")
    y = unpack_fp4(w1_words, w1_scales).T @ xq
    tg = f64(tscale)[:1][:, unstriped(offs)]
    return (f64(cscale) * y) * tg

@@ -1,0 +1,147 @@
+from contextlib import ExitStack
+
+import concourse.mybir as mybir
+from concourse.masks import make_identity
+
+K, T, S, N = 1024, 1024, 512, 256
+FLOPS = 2 * K * S * N
+
+F32 = mybir.dt.float32
+BF16 = mybir.dt.bfloat16
+I32 = mybir.dt.int32
+U32 = mybir.dt.uint32
+U16 = mybir.dt.uint16
+U8 = mybir.dt.uint8
+FP8X4 = mybir.dt.float8_e4m3fn_x4
+FP4X4 = mybir.dt.float4_e2m1fn_x4
+MULT = mybir.AluOpType.mult
+
+P = 128
+PASSES = 2
+HALF = T // 2
+SLICE = 128
+SLICES = S // SLICE
+M_TILES = N // P
+LAST_VECTOR_COLS = 352
+
+
+def tile_picked_tokscale_none_l_kernel(tc, xT, tscale, cscale, w1_words, w1_scales, offs, out):
+    nc = tc.nc
+    with ExitStack() as ctx:
+        keep = ctx.enter_context(tc.tile_pool(name="keep", bufs=1))
+        psum = ctx.enter_context(tc.psum_pool(name="psum", bufs=1))
+
+        offsets = keep.tile([P, S // 16], U16, name="offsets")
+        t_row = keep.tile([P, T], F32, name="t_row")
+        nc.scalar.dma_start(out=t_row[P - 1 : P, :], in_=tscale[0:1, :])
+        nc.vector.memset(t_row[0 : P - 1, :], 0.0)
+
+        raw = {}
+        for g in range(PASSES):
+            rows = xT[512 * g : 512 * (g + 1), :].rearrange("(p t) c -> p t c", t=4)
+            for u in range(2):
+                for h in range(2):
+                    raw[g, u, h] = keep.tile([P, 2, HALF], F32, name="raw%d%d%d" % (g, u, h))
+                    nc.sync.dma_start(out=raw[g, u, h][:], in_=rows[:, 2 * u : 2 * u + 2, h * HALF : (h + 1) * HALF])
+                    if (g, u, h) == (0, 0, 0):
+                        nc.sync.dma_start(offsets[:], offs)
+        w_words = keep.tile([P, PASSES, 2 * N], U8, name="w_words", align_bytes=64)
+        nc.sync.dma_start(out=w_words[:].bitcast(I32), in_=w1_words.rearrange("g p n -> p g n").bitcast(I32))
+
+        ident = keep.tile([P, P], F32, name="ident")
+        make_identity(nc, ident[:])
+        w_scales = keep.tile([P, PASSES, N], U8, name="w_scales", align_bytes=64)
+        nc.gpsimd.memset(w_scales[:].bitcast(I32), 0)
+        for q in range(4):
+            nc.gpsimd.dma_start(
+                out=w_scales[32 * q : 32 * q + 4, :, :].bitcast(I32),
+                in_=w1_scales[:, 4 * q : 4 * q + 4, :].rearrange("g r n -> r g n").bitcast(I32),
+            )
+        c_cols = keep.tile([P, M_TILES], F32, name="c_cols")
+        with nc.allow_non_contiguous_dma(reason="one channel scale for each partition"):
+            nc.gpsimd.dma_start(out=c_cols[:], in_=cscale.rearrange("(m p) o -> p (m o)", p=P))
+
+        t_last = keep.tile([P, S], F32, name="t_last")
+        nc.vector.tensor_copy(t_last[:], t_row[:].indirect(offsets[:]))
+        turned = psum.tile([P, SLICES, P], F32, name="turned", tag="bank0")
+        for s in range(SLICES):
+            nc.tensor.transpose(turned[:, s, :], t_last[:, s * P : (s + 1) * P], ident[:])
+        t_cols = keep.tile([P, SLICES], F32, name="t_cols")
+        nc.scalar.copy(out=t_cols[:], in_=turned[:, :, P - 1])
+        spread = psum.tile([P, SLICES, P], F32, name="spread", tag="bank1")
+        for s in range(SLICES):
+            nc.tensor.transpose(spread[:, s, :], t_cols[:, s : s + 1].to_broadcast([P, P]), ident[:])
+        t_picked = keep.tile([P, S], F32, name="t_picked")
+        nc.scalar.copy(out=t_picked[:], in_=spread[:].rearrange("q s p -> q (s p)"))
+
+        def cast(engine_copy, pairs, src, h, lo, hi):
+            view = pairs[:].bitcast(BF16).rearrange("p (c e) -> p c e", e=2)
+            engine_copy(out=view[:, h * HALF + lo : h * HALF + hi, :], in_=src[:, :, lo:hi].rearrange("p e c -> p c e"))
+
+        pairs = {}
+        picked = {}
+        for g in range(PASSES):
+            picked[g] = keep.tile([P, 2, S], U32, name="picked%d" % g)
+        acc = {}
+
+        def multiply(g, s, codes, scales):
+            for m in range(M_TILES):
+                if g == 0:
+                    acc[s, m] = psum.tile([P, SLICE], F32, name="acc%d%d" % (s, m), tag="bank%d" % (7 - (2 * s + m)))
+                nc.tensor.matmul_mx(
+                    out=acc[s, m][:],
+                    lhsT=w_words[:, g, 2 * P * m : 2 * P * (m + 1)].bitcast(FP4X4),
+                    lhsT_scale=w_scales[:, g, P * m : P * (m + 1)],
+                    rhs=codes.bitcast(FP8X4),
+                    rhs_scale=scales,
+                    start=(g == 0),
+                    stop=(g == PASSES - 1),
+                )
+
+        for g in range(PASSES):
+            for u in range(2):
+                pairs[g, u] = keep.tile([P, T], U32, name="pairs%d%d" % (g, u))
+                cast(nc.scalar.copy, pairs[g, u], raw[g, u, 0], 0, 0, HALF)
+                cast(nc.vector.tensor_copy, pairs[g, u], raw[g, u, 1], 1, 0, LAST_VECTOR_COLS)
+                cast(nc.scalar.copy, pairs[g, u], raw[g, u, 1], 1, LAST_VECTOR_COLS, HALF)
+                if (g, u) != (1, 1):
+                    nc.vector.tensor_copy(picked[g][:, u, :], pairs[g, u][:].indirect(offsets[:]))
+                if (g, u) == (0, 1):
+                    woven0 = keep.tile([P, S, 2], U32, name="woven0", align_bytes=64)
+                    nc.vector.tensor_copy(out=woven0[:].bitcast(I32), in_=picked[0][:].bitcast(I32).rearrange("p u j -> p j u"))
+                if (g, u) == (1, 0):
+                    codes0 = keep.tile([P, S], U32, name="codes0", align_bytes=64)
+                    scales0 = keep.tile([P, S], U8, name="scales0", align_bytes=64)
+                    nc.vector.quantize_mx(
+                        out=codes0[:].bitcast(FP8X4),
+                        scales=scales0[:],
+                        in_=woven0[:].rearrange("p j u -> p (j u)").bitcast(BF16),
+                    )
+                    for s in range(SLICES):
+                        cols = slice(s * SLICE, (s + 1) * SLICE)
+                        multiply(0, s, codes0[:, cols], scales0[:, cols])
+
+        woven = {}
+        for s in range(SLICES):
+            cols = slice(s * SLICE, (s + 1) * SLICE)
+            nc.vector.tensor_copy(picked[1][:, 1, cols], pairs[1, 1][:].indirect(offsets[:, 8 * s : 8 * (s + 1)]))
+            woven[s] = keep.tile([P, SLICE, 2], U32, name="woven1%d" % s, align_bytes=64)
+            nc.scalar.copy(out=woven[s][:], in_=picked[1][:, :, cols].rearrange("p u j -> p j u"))
+        for s in range(SLICES):
+            codes = keep.tile([P, SLICE], U32, name="codes1%d" % s, align_bytes=64)
+            scales = keep.tile([P, SLICE], U8, name="scales1%d" % s, align_bytes=64)
+            nc.vector.quantize_mx(
+                out=codes[:].bitcast(FP8X4),
+                scales=scales[:],
+                in_=woven[s][:].rearrange("p j u -> p (j u)").bitcast(BF16),
+            )
+            multiply(1, s, codes[:], scales[:])
+        out3 = out.rearrange("(m p) j -> p m j", p=P)
+        for s in range(SLICES):
+            cols = slice(s * SLICE, (s + 1) * SLICE)
+            result = keep.tile([P, M_TILES, SLICE], F32, name="result%d" % s)
+            for m in range(M_TILES):
+                nc.vector.scalar_tensor_tensor(
+                    out=result[:, m, :], in0=acc[s, m][:], scalar=c_cols[:, m : m + 1], in1=t_picked[:, cols], op0=MULT, op1=MULT
+                )
+            nc.sync.dma_start(out=out3[:, :, cols], in_=result[:])

@@ -22,7 +22,7 @@ HALF = T // 2
 SLICE = 128
 SLICES = S // SLICE
 M_TILES = N // P
-LAST_VECTOR_COLS = 352
+VECTOR_COLS = {(0, 0): 352, (0, 1): 352, (1, 0): 160, (1, 1): 352}
 
 
 def tile_picked_tokscale_none_l_kernel(tc, xT, tscale, cscale, w1_words, w1_scales, offs, out):
@@ -48,18 +48,18 @@ def tile_picked_tokscale_none_l_kernel(tc, xT, tscale, cscale, w1_words, w1_scal
         w_words = keep.tile([P, PASSES, 2 * N], U8, name="w_words", align_bytes=64)
         nc.sync.dma_start(out=w_words[:].bitcast(I32), in_=w1_words.rearrange("g p n -> p g n").bitcast(I32))
 
-        ident = keep.tile([P, P], F32, name="ident")
-        make_identity(nc, ident[:])
         w_scales = keep.tile([P, PASSES, N], U8, name="w_scales", align_bytes=64)
         nc.gpsimd.memset(w_scales[:].bitcast(I32), 0)
+        ident = keep.tile([P, P], F32, name="ident")
+        make_identity(nc, ident[:])
         for q in range(4):
-            nc.gpsimd.dma_start(
+            nc.sync.dma_start(
                 out=w_scales[32 * q : 32 * q + 4, :, :].bitcast(I32),
                 in_=w1_scales[:, 4 * q : 4 * q + 4, :].rearrange("g r n -> r g n").bitcast(I32),
             )
         c_cols = keep.tile([P, M_TILES], F32, name="c_cols")
         with nc.allow_non_contiguous_dma(reason="one channel scale for each partition"):
-            nc.gpsimd.dma_start(out=c_cols[:], in_=cscale.rearrange("(m p) o -> p (m o)", p=P))
+            nc.sync.dma_start(out=c_cols[:], in_=cscale.rearrange("(m p) o -> p (m o)", p=P))
 
         t_last = keep.tile([P, S], F32, name="t_last")
         nc.vector.tensor_copy(t_last[:], t_row[:].indirect(offsets[:]))
@@ -75,8 +75,11 @@ def tile_picked_tokscale_none_l_kernel(tc, xT, tscale, cscale, w1_words, w1_scal
         nc.scalar.copy(out=t_picked[:], in_=spread[:].rearrange("q s p -> q (s p)"))
 
         def cast(engine_copy, pairs, src, h, lo, hi):
-            view = pairs[:].bitcast(BF16).rearrange("p (c e) -> p c e", e=2)
-            engine_copy(out=view[:, h * HALF + lo : h * HALF + hi, :], in_=src[:, :, lo:hi].rearrange("p e c -> p c e"))
+            view = pairs[:, h * HALF + lo : h * HALF + hi].bitcast(BF16).rearrange("p (c i e) -> p c e i", i=4, e=2)
+            engine_copy(out=view, in_=src[:, :, lo:hi].rearrange("p e (c i) -> p c e i", i=4))
+
+        def weave(engine_copy, dst, src):
+            engine_copy(out=dst.rearrange("p (c i u) -> p c u i", i=4, u=2), in_=src.rearrange("p u (c i) -> p c u i", i=4))
 
         pairs = {}
         picked = {}
@@ -102,38 +105,38 @@ def tile_picked_tokscale_none_l_kernel(tc, xT, tscale, cscale, w1_words, w1_scal
             for u in range(2):
                 pairs[g, u] = keep.tile([P, T], U32, name="pairs%d%d" % (g, u))
                 cast(nc.scalar.copy, pairs[g, u], raw[g, u, 0], 0, 0, HALF)
-                cast(nc.vector.tensor_copy, pairs[g, u], raw[g, u, 1], 1, 0, LAST_VECTOR_COLS)
-                cast(nc.scalar.copy, pairs[g, u], raw[g, u, 1], 1, LAST_VECTOR_COLS, HALF)
-                if (g, u) != (1, 1):
+                cast(nc.vector.tensor_copy, pairs[g, u], raw[g, u, 1], 1, 0, VECTOR_COLS[g, u])
+                cast(nc.scalar.copy, pairs[g, u], raw[g, u, 1], 1, VECTOR_COLS[g, u], HALF)
+                if u == 0:
                     nc.vector.tensor_copy(picked[g][:, u, :], pairs[g, u][:].indirect(offsets[:]))
                 if (g, u) == (0, 1):
-                    woven0 = keep.tile([P, S, 2], U32, name="woven0", align_bytes=64)
-                    nc.vector.tensor_copy(out=woven0[:].bitcast(I32), in_=picked[0][:].bitcast(I32).rearrange("p u j -> p j u"))
-                if (g, u) == (1, 0):
-                    codes0 = keep.tile([P, S], U32, name="codes0", align_bytes=64)
-                    scales0 = keep.tile([P, S], U8, name="scales0", align_bytes=64)
-                    nc.vector.quantize_mx(
-                        out=codes0[:].bitcast(FP8X4),
-                        scales=scales0[:],
-                        in_=woven0[:].rearrange("p j u -> p (j u)").bitcast(BF16),
-                    )
-                    for s in range(SLICES):
-                        cols = slice(s * SLICE, (s + 1) * SLICE)
-                        multiply(0, s, codes0[:, cols], scales0[:, cols])
+                    woven0 = {}
+                    for b in range(2):
+                        nc.vector.tensor_copy(picked[0][:, 1, 256 * b : 256 * (b + 1)], pairs[0, 1][:].indirect(offsets[:, 16 * b : 16 * (b + 1)]))
+                    for b in range(2):
+                        woven0[b] = keep.tile([P, 512], U32, name="woven0%d" % b, align_bytes=64)
+                        weave(nc.vector.tensor_copy, woven0[b][:].bitcast(I32), picked[0][:, :, 256 * b : 256 * (b + 1)].bitcast(I32))
+                    for b in range(2):
+                        codes0 = keep.tile([P, 256], U32, name="codes0%d" % b, align_bytes=64)
+                        scales0 = keep.tile([P, 256], U8, name="scales0%d" % b, align_bytes=64)
+                        nc.vector.quantize_mx(out=codes0[:].bitcast(FP8X4), scales=scales0[:], in_=woven0[b][:].bitcast(BF16))
+                        for s in range(2):
+                            cols = slice(s * SLICE, (s + 1) * SLICE)
+                            multiply(0, 2 * b + s, codes0[:, cols], scales0[:, cols])
 
         woven = {}
         for s in range(SLICES):
             cols = slice(s * SLICE, (s + 1) * SLICE)
             nc.vector.tensor_copy(picked[1][:, 1, cols], pairs[1, 1][:].indirect(offsets[:, 8 * s : 8 * (s + 1)]))
-            woven[s] = keep.tile([P, SLICE, 2], U32, name="woven1%d" % s, align_bytes=64)
-            nc.scalar.copy(out=woven[s][:], in_=picked[1][:, :, cols].rearrange("p u j -> p j u"))
+            woven[s] = keep.tile([P, 2 * SLICE], U32, name="woven1%d" % s, align_bytes=64)
+            weave(nc.scalar.copy, woven[s][:], picked[1][:, :, cols])
         for s in range(SLICES):
             codes = keep.tile([P, SLICE], U32, name="codes1%d" % s, align_bytes=64)
             scales = keep.tile([P, SLICE], U8, name="scales1%d" % s, align_bytes=64)
             nc.vector.quantize_mx(
                 out=codes[:].bitcast(FP8X4),
                 scales=scales[:],
-                in_=woven[s][:].rearrange("p j u -> p (j u)").bitcast(BF16),
+                in_=woven[s][:].bitcast(BF16),
             )
             multiply(1, s, codes[:], scales[:])
         out3 = out.rearrange("(m p) j -> p m j", p=P)

@@ -17,12 +17,29 @@ FP4X4 = mybir.dt.float4_e2m1fn_x4
 MULT = mybir.AluOpType.mult
 
 P = 128
-PASSES = 2
+K_PASS = 4 * P
+PASSES = K // K_PASS
+PER_COLUMN = 16
 HALF = T // 2
 SLICE = 128
 SLICES = S // SLICE
 M_TILES = N // P
-VECTOR_COLS = {(0, 0): 352, (0, 1): 352, (1, 0): 160, (1, 1): 352}
+BANKS = SLICES * M_TILES
+LINE = 4
+VECTOR_SHARE = 352
+VECTOR_SHARE_THIRD = 256
+
+
+def cast_pairs(copy, pairs, rows, first, lo, hi):
+    halves = pairs[:, first + lo : first + hi].bitcast(BF16)
+    copy(
+        out=halves.rearrange("p (c i e) -> p c e i", i=LINE, e=2),
+        in_=rows[:, :, lo:hi].rearrange("p e (c i) -> p c e i", i=LINE),
+    )
+
+
+def entries(offsets, lo, hi):
+    return offsets[:, lo // PER_COLUMN : hi // PER_COLUMN]
 
 
 def tile_picked_tokscale_none_l_kernel(tc, xT, tscale, cscale, w1_words, w1_scales, offs, out):
@@ -31,23 +48,22 @@ def tile_picked_tokscale_none_l_kernel(tc, xT, tscale, cscale, w1_words, w1_scal
         keep = ctx.enter_context(tc.tile_pool(name="keep", bufs=1))
         psum = ctx.enter_context(tc.psum_pool(name="psum", bufs=1))
 
-        offsets = keep.tile([P, S // 16], U16, name="offsets")
+        offsets = keep.tile([P, S // PER_COLUMN], U16, name="offsets")
+        nc.sync.dma_start(offsets[:], offs)
         t_row = keep.tile([P, T], F32, name="t_row")
         nc.scalar.dma_start(out=t_row[P - 1 : P, :], in_=tscale[0:1, :])
         nc.vector.memset(t_row[0 : P - 1, :], 0.0)
 
         raw = {}
         for g in range(PASSES):
-            rows = xT[512 * g : 512 * (g + 1), :].rearrange("(p t) c -> p t c", t=4)
+            rows = xT[K_PASS * g : K_PASS * (g + 1), :].rearrange("(p t) c -> p t c", t=4)
             for u in range(2):
                 for h in range(2):
                     raw[g, u, h] = keep.tile([P, 2, HALF], F32, name="raw%d%d%d" % (g, u, h))
                     nc.sync.dma_start(out=raw[g, u, h][:], in_=rows[:, 2 * u : 2 * u + 2, h * HALF : (h + 1) * HALF])
-                    if (g, u, h) == (0, 0, 0):
-                        nc.sync.dma_start(offsets[:], offs)
+
         w_words = keep.tile([P, PASSES, 2 * N], U8, name="w_words", align_bytes=64)
         nc.sync.dma_start(out=w_words[:].bitcast(I32), in_=w1_words.rearrange("g p n -> p g n").bitcast(I32))
-
         w_scales = keep.tile([P, PASSES, N], U8, name="w_scales", align_bytes=64)
         nc.gpsimd.memset(w_scales[:].bitcast(I32), 0)
         ident = keep.tile([P, P], F32, name="ident")
@@ -67,30 +83,31 @@ def tile_picked_tokscale_none_l_kernel(tc, xT, tscale, cscale, w1_words, w1_scal
         for s in range(SLICES):
             nc.tensor.transpose(turned[:, s, :], t_last[:, s * P : (s + 1) * P], ident[:])
         t_cols = keep.tile([P, SLICES], F32, name="t_cols")
-        nc.scalar.copy(out=t_cols[:], in_=turned[:, :, P - 1])
+        nc.vector.tensor_copy(out=t_cols[:], in_=turned[:, :, P - 1])
         spread = psum.tile([P, SLICES, P], F32, name="spread", tag="bank1")
         for s in range(SLICES):
             nc.tensor.transpose(spread[:, s, :], t_cols[:, s : s + 1].to_broadcast([P, P]), ident[:])
-        t_picked = keep.tile([P, S], F32, name="t_picked")
-        nc.scalar.copy(out=t_picked[:], in_=spread[:].rearrange("q s p -> q (s p)"))
 
-        def cast(engine_copy, pairs, src, h, lo, hi):
-            view = pairs[:, h * HALF + lo : h * HALF + hi].bitcast(BF16).rearrange("p (c i e) -> p c e i", i=4, e=2)
-            engine_copy(out=view, in_=src[:, :, lo:hi].rearrange("p e (c i) -> p c e i", i=4))
+        def make_pairs(g, u, vector_share):
+            pairs = keep.tile([P, T], U32, name="pairs%d%d" % (g, u))
+            cast_pairs(nc.scalar.copy, pairs, raw[g, u, 0], 0, 0, HALF)
+            cast_pairs(nc.vector.tensor_copy, pairs, raw[g, u, 1], HALF, 0, vector_share)
+            cast_pairs(nc.scalar.copy, pairs, raw[g, u, 1], HALF, vector_share, HALF)
+            return pairs
 
-        def weave(engine_copy, dst, src):
-            engine_copy(out=dst.rearrange("p (c i u) -> p c u i", i=4, u=2), in_=src.rearrange("p u (c i) -> p c u i", i=4))
+        def quantise(woven, width, name):
+            codes = keep.tile([P, width], U32, name="codes" + name, align_bytes=64)
+            scales = keep.tile([P, width], U8, name="scales" + name, align_bytes=64)
+            nc.vector.quantize_mx(out=codes[:].bitcast(FP8X4), scales=scales[:], in_=woven.bitcast(BF16))
+            return codes, scales
 
-        pairs = {}
-        picked = {}
-        for g in range(PASSES):
-            picked[g] = keep.tile([P, 2, S], U32, name="picked%d" % g)
         acc = {}
 
         def multiply(g, s, codes, scales):
             for m in range(M_TILES):
                 if g == 0:
-                    acc[s, m] = psum.tile([P, SLICE], F32, name="acc%d%d" % (s, m), tag="bank%d" % (7 - (2 * s + m)))
+                    bank = BANKS - 1 - (M_TILES * s + m)
+                    acc[s, m] = psum.tile([P, SLICE], F32, name="acc%d%d" % (s, m), tag="bank%d" % bank)
                 nc.tensor.matmul_mx(
                     out=acc[s, m][:],
                     lhsT=w_words[:, g, 2 * P * m : 2 * P * (m + 1)].bitcast(FP4X4),
@@ -101,50 +118,53 @@ def tile_picked_tokscale_none_l_kernel(tc, xT, tscale, cscale, w1_words, w1_scal
                     stop=(g == PASSES - 1),
                 )
 
-        for g in range(PASSES):
-            for u in range(2):
-                pairs[g, u] = keep.tile([P, T], U32, name="pairs%d%d" % (g, u))
-                cast(nc.scalar.copy, pairs[g, u], raw[g, u, 0], 0, 0, HALF)
-                cast(nc.vector.tensor_copy, pairs[g, u], raw[g, u, 1], 1, 0, VECTOR_COLS[g, u])
-                cast(nc.scalar.copy, pairs[g, u], raw[g, u, 1], 1, VECTOR_COLS[g, u], HALF)
-                if u == 0:
-                    nc.vector.tensor_copy(picked[g][:, u, :], pairs[g, u][:].indirect(offsets[:]))
-                if (g, u) == (0, 1):
-                    woven0 = {}
-                    for b in range(2):
-                        nc.vector.tensor_copy(picked[0][:, 1, 256 * b : 256 * (b + 1)], pairs[0, 1][:].indirect(offsets[:, 16 * b : 16 * (b + 1)]))
-                    for b in range(2):
-                        woven0[b] = keep.tile([P, 512], U32, name="woven0%d" % b, align_bytes=64)
-                        weave(nc.vector.tensor_copy, woven0[b][:].bitcast(I32), picked[0][:, :, 256 * b : 256 * (b + 1)].bitcast(I32))
-                    for b in range(2):
-                        codes0 = keep.tile([P, 256], U32, name="codes0%d" % b, align_bytes=64)
-                        scales0 = keep.tile([P, 256], U8, name="scales0%d" % b, align_bytes=64)
-                        nc.vector.quantize_mx(out=codes0[:].bitcast(FP8X4), scales=scales0[:], in_=woven0[b][:].bitcast(BF16))
-                        for s in range(2):
-                            cols = slice(s * SLICE, (s + 1) * SLICE)
-                            multiply(0, 2 * b + s, codes0[:, cols], scales0[:, cols])
+        picked = keep.tile([P, SLICES, 2, SLICE], U32, name="picked")
+        pairs = make_pairs(0, 0, VECTOR_SHARE)
+        woven_all = keep.tile([P, S, 2], U32, name="woven_all", align_bytes=64)
+        nc.vector.tensor_copy(woven_all[:, :, 0], pairs[:].indirect(offsets[:]))
+        pairs = make_pairs(0, 1, VECTOR_SHARE)
+        halves = [(0, S // 2), (S // 2, S)]
+        for lo, hi in halves:
+            nc.vector.tensor_copy(woven_all[:, lo:hi, 1], pairs[:].indirect(entries(offsets, lo, hi)))
+        for lo, hi in halves:
+            codes, scales = quantise(woven_all[:, lo:hi, :].rearrange("p j u -> p (j u)"), hi - lo, "0_%d" % lo)
+            for first in range(0, hi - lo, SLICE):
+                cols = slice(first, first + SLICE)
+                multiply(0, (lo + first) // SLICE, codes[:, cols], scales[:, cols])
+
+        pairs = make_pairs(1, 0, VECTOR_SHARE_THIRD)
+        nc.vector.tensor_copy(picked[:, :, 0, :], pairs[:].indirect(offsets[:]))
+        pairs = make_pairs(1, 1, VECTOR_SHARE)
+        t_picked = keep.tile([P, S], F32, name="t_picked", tag="raw111")
+        nc.scalar.copy(out=t_picked[:], in_=spread[:].rearrange("q s p -> q (s p)"))
 
         woven = {}
         for s in range(SLICES):
-            cols = slice(s * SLICE, (s + 1) * SLICE)
-            nc.vector.tensor_copy(picked[1][:, 1, cols], pairs[1, 1][:].indirect(offsets[:, 8 * s : 8 * (s + 1)]))
-            woven[s] = keep.tile([P, 2 * SLICE], U32, name="woven1%d" % s, align_bytes=64)
-            weave(nc.scalar.copy, woven[s][:], picked[1][:, :, cols])
-        for s in range(SLICES):
-            codes = keep.tile([P, SLICE], U32, name="codes1%d" % s, align_bytes=64)
-            scales = keep.tile([P, SLICE], U8, name="scales1%d" % s, align_bytes=64)
-            nc.vector.quantize_mx(
-                out=codes[:].bitcast(FP8X4),
-                scales=scales[:],
-                in_=woven[s][:].bitcast(BF16),
+            nc.vector.tensor_copy(picked[:, s, 1, :], pairs[:].indirect(entries(offsets, s * SLICE, (s + 1) * SLICE)))
+            woven[s] = keep.tile([P, 2 * SLICE], U32, name="woven%d" % s, align_bytes=64)
+            nc.scalar.copy(
+                out=woven[s][:].rearrange("p (c i u) -> p c u i", i=LINE, u=2),
+                in_=picked[:, s, :, :].rearrange("p u (c i) -> p c u i", i=LINE),
             )
+        for s in range(SLICES):
+            codes, scales = quantise(woven[s][:], SLICE, "1_%d" % s)
             multiply(1, s, codes[:], scales[:])
-        out3 = out.rearrange("(m p) j -> p m j", p=P)
+
+        out_tiles = out.rearrange("(m p) j -> p m j", p=P)
         for s in range(SLICES):
             cols = slice(s * SLICE, (s + 1) * SLICE)
+            last = s == SLICES - 1
             result = keep.tile([P, M_TILES, SLICE], F32, name="result%d" % s)
             for m in range(M_TILES):
                 nc.vector.scalar_tensor_tensor(
-                    out=result[:, m, :], in0=acc[s, m][:], scalar=c_cols[:, m : m + 1], in1=t_picked[:, cols], op0=MULT, op1=MULT
+                    out=result[:, m, :],
+                    in0=acc[s, m][:],
+                    scalar=c_cols[:, m : m + 1],
+                    in1=t_picked[:, cols],
+                    op0=MULT,
+                    op1=MULT,
                 )
-            nc.sync.dma_start(out=out3[:, :, cols], in_=result[:])
+                if last:
+                    nc.sync.dma_start(out=out_tiles[:, m, cols], in_=result[:, m, :])
+            if not last:
+                nc.sync.dma_start(out=out_tiles[:, :, cols], in_=result[:])

@@ -27,7 +27,7 @@ M_TILES = N // P
 BANKS = SLICES * M_TILES
 LINE = 4
 VECTOR_SHARE = 352
-VECTOR_SHARE_THIRD = 256
+VECTOR_SHARE_THIRD = 160
 
 
 def cast_pairs(copy, pairs, rows, first, lo, hi):
@@ -35,6 +35,13 @@ def cast_pairs(copy, pairs, rows, first, lo, hi):
     copy(
         out=halves.rearrange("p (c i e) -> p c e i", i=LINE, e=2),
         in_=rows[:, :, lo:hi].rearrange("p e (c i) -> p c e i", i=LINE),
+    )
+
+
+def weave(copy, woven, picked):
+    copy(
+        out=woven.rearrange("p (c i u) -> p c u i", i=LINE, u=2),
+        in_=picked.rearrange("p u (c i) -> p c u i", i=LINE),
     )
 
 
@@ -49,7 +56,6 @@ def tile_picked_tokscale_none_l_kernel(tc, xT, tscale, cscale, w1_words, w1_scal
         psum = ctx.enter_context(tc.psum_pool(name="psum", bufs=1))
 
         offsets = keep.tile([P, S // PER_COLUMN], U16, name="offsets")
-        nc.sync.dma_start(offsets[:], offs)
         t_row = keep.tile([P, T], F32, name="t_row")
         nc.scalar.dma_start(out=t_row[P - 1 : P, :], in_=tscale[0:1, :])
         nc.vector.memset(t_row[0 : P - 1, :], 0.0)
@@ -61,6 +67,8 @@ def tile_picked_tokscale_none_l_kernel(tc, xT, tscale, cscale, w1_words, w1_scal
                 for h in range(2):
                     raw[g, u, h] = keep.tile([P, 2, HALF], F32, name="raw%d%d%d" % (g, u, h))
                     nc.sync.dma_start(out=raw[g, u, h][:], in_=rows[:, 2 * u : 2 * u + 2, h * HALF : (h + 1) * HALF])
+                    if (g, u, h) == (0, 0, 0):
+                        nc.sync.dma_start(offsets[:], offs)
 
         w_words = keep.tile([P, PASSES, 2 * N], U8, name="w_words", align_bytes=64)
         nc.sync.dma_start(out=w_words[:].bitcast(I32), in_=w1_words.rearrange("g p n -> p g n").bitcast(I32))
@@ -69,7 +77,7 @@ def tile_picked_tokscale_none_l_kernel(tc, xT, tscale, cscale, w1_words, w1_scal
         ident = keep.tile([P, P], F32, name="ident")
         make_identity(nc, ident[:])
         for q in range(4):
-            nc.sync.dma_start(
+            nc.gpsimd.dma_start(
                 out=w_scales[32 * q : 32 * q + 4, :, :].bitcast(I32),
                 in_=w1_scales[:, 4 * q : 4 * q + 4, :].rearrange("g r n -> r g n").bitcast(I32),
             )
@@ -83,10 +91,12 @@ def tile_picked_tokscale_none_l_kernel(tc, xT, tscale, cscale, w1_words, w1_scal
         for s in range(SLICES):
             nc.tensor.transpose(turned[:, s, :], t_last[:, s * P : (s + 1) * P], ident[:])
         t_cols = keep.tile([P, SLICES], F32, name="t_cols")
-        nc.vector.tensor_copy(out=t_cols[:], in_=turned[:, :, P - 1])
+        nc.scalar.copy(out=t_cols[:], in_=turned[:, :, P - 1])
         spread = psum.tile([P, SLICES, P], F32, name="spread", tag="bank1")
         for s in range(SLICES):
             nc.tensor.transpose(spread[:, s, :], t_cols[:, s : s + 1].to_broadcast([P, P]), ident[:])
+        t_picked = keep.tile([P, S], F32, name="t_picked")
+        nc.scalar.copy(out=t_picked[:], in_=spread[:].rearrange("q s p -> q (s p)"))
 
         def make_pairs(g, u, vector_share):
             pairs = keep.tile([P, T], U32, name="pairs%d%d" % (g, u))
@@ -118,37 +128,35 @@ def tile_picked_tokscale_none_l_kernel(tc, xT, tscale, cscale, w1_words, w1_scal
                     stop=(g == PASSES - 1),
                 )
 
-        picked = keep.tile([P, SLICES, 2, SLICE], U32, name="picked")
+        picked = [keep.tile([P, 2, S], U32, name="picked%d" % g) for g in range(PASSES)]
         pairs = make_pairs(0, 0, VECTOR_SHARE)
-        woven_all = keep.tile([P, S, 2], U32, name="woven_all", align_bytes=64)
-        nc.vector.tensor_copy(woven_all[:, :, 0], pairs[:].indirect(offsets[:]))
+        nc.vector.tensor_copy(picked[0][:, 0, :], pairs[:].indirect(offsets[:]))
         pairs = make_pairs(0, 1, VECTOR_SHARE)
         halves = [(0, S // 2), (S // 2, S)]
         for lo, hi in halves:
-            nc.vector.tensor_copy(woven_all[:, lo:hi, 1], pairs[:].indirect(entries(offsets, lo, hi)))
+            nc.vector.tensor_copy(picked[0][:, 1, lo:hi], pairs[:].indirect(entries(offsets, lo, hi)))
+        woven = {}
         for lo, hi in halves:
-            codes, scales = quantise(woven_all[:, lo:hi, :].rearrange("p j u -> p (j u)"), hi - lo, "0_%d" % lo)
-            for first in range(0, hi - lo, SLICE):
-                cols = slice(first, first + SLICE)
-                multiply(0, (lo + first) // SLICE, codes[:, cols], scales[:, cols])
+            woven[lo] = keep.tile([P, 2 * (hi - lo)], U32, name="woven0_%d" % lo, align_bytes=64)
+            weave(nc.vector.tensor_copy, woven[lo][:].bitcast(I32), picked[0][:, :, lo:hi].bitcast(I32))
+        for lo, hi in halves:
+            codes, scales = quantise(woven[lo][:], hi - lo, "0_%d" % lo)
+            for first in range(lo, hi, SLICE):
+                cols = slice(first - lo, first - lo + SLICE)
+                multiply(0, first // SLICE, codes[:, cols], scales[:, cols])
 
         pairs = make_pairs(1, 0, VECTOR_SHARE_THIRD)
-        nc.vector.tensor_copy(picked[:, :, 0, :], pairs[:].indirect(offsets[:]))
+        nc.vector.tensor_copy(picked[1][:, 0, :], pairs[:].indirect(offsets[:]))
         pairs = make_pairs(1, 1, VECTOR_SHARE)
-        t_picked = keep.tile([P, S], F32, name="t_picked", tag="raw111")
-        nc.scalar.copy(out=t_picked[:], in_=spread[:].rearrange("q s p -> q (s p)"))
 
-        woven = {}
-        for s in range(SLICES):
-            nc.vector.tensor_copy(picked[:, s, 1, :], pairs[:].indirect(entries(offsets, s * SLICE, (s + 1) * SLICE)))
-            woven[s] = keep.tile([P, 2 * SLICE], U32, name="woven%d" % s, align_bytes=64)
-            nc.scalar.copy(
-                out=woven[s][:].rearrange("p (c i u) -> p c u i", i=LINE, u=2),
-                in_=picked[:, s, :, :].rearrange("p u (c i) -> p c u i", i=LINE),
-            )
-        for s in range(SLICES):
-            codes, scales = quantise(woven[s][:], SLICE, "1_%d" % s)
-            multiply(1, s, codes[:], scales[:])
+        starts = range(0, S, SLICE)
+        for lo in starts:
+            nc.vector.tensor_copy(picked[1][:, 1, lo : lo + SLICE], pairs[:].indirect(entries(offsets, lo, lo + SLICE)))
+            woven[lo] = keep.tile([P, 2 * SLICE], U32, name="woven1_%d" % lo, align_bytes=64)
+            weave(nc.scalar.copy, woven[lo][:], picked[1][:, :, lo : lo + SLICE])
+        for lo in starts:
+            codes, scales = quantise(woven[lo][:], SLICE, "1_%d" % lo)
+            multiply(1, lo // SLICE, codes[:], scales[:])
 
         out_tiles = out.rearrange("(m p) j -> p m j", p=P)
         for s in range(SLICES):

@@ -77,7 +77,7 @@ def tile_picked_tokscale_none_l_kernel(tc, xT, tscale, cscale, w1_words, w1_scal
         ident = keep.tile([P, P], F32, name="ident")
         make_identity(nc, ident[:])
         for q in range(4):
-            nc.gpsimd.dma_start(
+            nc.sync.dma_start(
                 out=w_scales[32 * q : 32 * q + 4, :, :].bitcast(I32),
                 in_=w1_scales[:, 4 * q : 4 * q + 4, :].rearrange("g r n -> r g n").bitcast(I32),
             )
@@ -158,6 +158,7 @@ def tile_picked_tokscale_none_l_kernel(tc, xT, tscale, cscale, w1_words, w1_scal
             codes, scales = quantise(woven[lo][:], SLICE, "1_%d" % lo)
             multiply(1, lo // SLICE, codes[:], scales[:])
 
+        queues = (nc.sync, nc.scalar)
         out_tiles = out.rearrange("(m p) j -> p m j", p=P)
         for s in range(SLICES):
             cols = slice(s * SLICE, (s + 1) * SLICE)
@@ -173,6 +174,6 @@ def tile_picked_tokscale_none_l_kernel(tc, xT, tscale, cscale, w1_words, w1_scal
                     op1=MULT,
                 )
                 if last:
-                    nc.sync.dma_start(out=out_tiles[:, m, cols], in_=result[:, m, :])
+                    queues[(s + m) % 2].dma_start(out=out_tiles[:, m, cols], in_=result[:, m, :])
             if not last:
-                nc.sync.dma_start(out=out_tiles[:, :, cols], in_=result[:])
+                queues[s % 2].dma_start(out=out_tiles[:, :, cols], in_=result[:])

@@ -30,11 +30,10 @@ VECTOR_SHARE = 352
 VECTOR_SHARE_THIRD = 160
 
 
-def cast_pairs(copy, pairs, rows, first, lo, hi):
-    halves = pairs[:, first + lo : first + hi].bitcast(BF16)
+def cast_pairs(copy, pairs, rows):
     copy(
-        out=halves.rearrange("p (c i e) -> p c e i", i=LINE, e=2),
-        in_=rows[:, :, lo:hi].rearrange("p e (c i) -> p c e i", i=LINE),
+        out=pairs.bitcast(BF16).rearrange("p (c i e) -> p c e i", i=LINE, e=2),
+        in_=rows.rearrange("p e (c i) -> p c e i", i=LINE),
     )
 
 
@@ -56,54 +55,59 @@ def tile_picked_tokscale_none_l_kernel(tc, xT, tscale, cscale, w1_words, w1_scal
         psum = ctx.enter_context(tc.psum_pool(name="psum", bufs=1))
 
         offsets = keep.tile([P, S // PER_COLUMN], U16, name="offsets")
+        nc.sync.dma_start(offsets[:], offs)
         t_row = keep.tile([P, T], F32, name="t_row")
         nc.scalar.dma_start(out=t_row[P - 1 : P, :], in_=tscale[0:1, :])
         nc.vector.memset(t_row[0 : P - 1, :], 0.0)
 
-        raw = {}
-        for g in range(PASSES):
-            rows = xT[K_PASS * g : K_PASS * (g + 1), :].rearrange("(p t) c -> p t c", t=4)
-            for u in range(2):
-                for h in range(2):
-                    raw[g, u, h] = keep.tile([P, 2, HALF], F32, name="raw%d%d%d" % (g, u, h))
-                    nc.sync.dma_start(out=raw[g, u, h][:], in_=rows[:, 2 * u : 2 * u + 2, h * HALF : (h + 1) * HALF])
-                    if (g, u, h) == (0, 0, 0):
-                        nc.sync.dma_start(offsets[:], offs)
-
-        w_words = keep.tile([P, PASSES, 2 * N], U8, name="w_words", align_bytes=64)
-        nc.sync.dma_start(out=w_words[:].bitcast(I32), in_=w1_words.rearrange("g p n -> p g n").bitcast(I32))
+        w_words = [keep.tile([P, 2 * N], U8, name="w_words%d" % g, align_bytes=64) for g in range(PASSES)]
         w_scales = keep.tile([P, PASSES, N], U8, name="w_scales", align_bytes=64)
         nc.gpsimd.memset(w_scales[:].bitcast(I32), 0)
-        ident = keep.tile([P, P], F32, name="ident")
-        make_identity(nc, ident[:])
-        for q in range(4):
-            nc.sync.dma_start(
-                out=w_scales[32 * q : 32 * q + 4, :, :].bitcast(I32),
-                in_=w1_scales[:, 4 * q : 4 * q + 4, :].rearrange("g r n -> r g n").bitcast(I32),
-            )
+
+        first = {(n, h): HALF * h for n in range(4) for h in range(2)}
+        raw = {}
+        for n in range(4):
+            g, u = divmod(n, 2)
+            rows = xT[K_PASS * g : K_PASS * (g + 1), :].rearrange("(p t) c -> p t c", t=4)
+            for h in range(2):
+                raw[n, h] = keep.tile([P, 2, HALF], F32, name="raw%d%d" % (n, h), tag="raw%d%d" % (n, h), align_bytes=64)
+                nc.sync.dma_start(out=raw[n, h][:], in_=rows[:, 2 * u : 2 * u + 2, first[n, h] : first[n, h] + HALF])
+                if (n, h) == (2, 1):
+                    for q in range(4):
+                        nc.sync.dma_start(
+                            out=w_scales[32 * q : 32 * q + 4, :, :].bitcast(I32),
+                            in_=w1_scales[:, 4 * q : 4 * q + 4, :].rearrange("g r n -> r g n").bitcast(I32),
+                        )
+                    nc.sync.dma_start(out=w_words[0][:].bitcast(I32), in_=w1_words[0].bitcast(I32))
+        nc.sync.dma_start(out=w_words[1][:].bitcast(I32), in_=w1_words[1].bitcast(I32))
         c_cols = keep.tile([P, M_TILES], F32, name="c_cols")
         with nc.allow_non_contiguous_dma(reason="one channel scale for each partition"):
             nc.sync.dma_start(out=c_cols[:], in_=cscale.rearrange("(m p) o -> p (m o)", p=P))
+        ident = keep.tile([P, P], F32, name="ident")
+        make_identity(nc, ident[:])
+
+        windows = {}
+
+        def open_window(n, spare=0):
+            tag = "raw%d1" % (n - 1) if n else "window0"
+            windows[n] = keep.tile([P, T + spare], U32, name="window%d" % n, tag=tag, align_bytes=64)
+            return windows[n][:, T : T + spare].bitcast(F32) if spare else None
+
+        def window(n):
+            return windows[n][:, 0:T]
+
+        def cast(copy, n, h, lo, hi):
+            cast_pairs(copy, window(n)[:, first[n, h] + lo : first[n, h] + hi], raw[n, h][:, :, lo:hi])
+
+        def cast_shared(n, share=VECTOR_SHARE):
+            cast(nc.vector.tensor_copy, n, 1, 0, share)
+            cast(nc.scalar.copy, n, 1, share, HALF)
 
         t_last = keep.tile([P, S], F32, name="t_last")
         nc.vector.tensor_copy(t_last[:], t_row[:].indirect(offsets[:]))
         turned = psum.tile([P, SLICES, P], F32, name="turned", tag="bank0")
         for s in range(SLICES):
             nc.tensor.transpose(turned[:, s, :], t_last[:, s * P : (s + 1) * P], ident[:])
-        t_cols = keep.tile([P, SLICES], F32, name="t_cols")
-        nc.scalar.copy(out=t_cols[:], in_=turned[:, :, P - 1])
-        spread = psum.tile([P, SLICES, P], F32, name="spread", tag="bank1")
-        for s in range(SLICES):
-            nc.tensor.transpose(spread[:, s, :], t_cols[:, s : s + 1].to_broadcast([P, P]), ident[:])
-        t_picked = keep.tile([P, S], F32, name="t_picked")
-        nc.scalar.copy(out=t_picked[:], in_=spread[:].rearrange("q s p -> q (s p)"))
-
-        def make_pairs(g, u, vector_share):
-            pairs = keep.tile([P, T], U32, name="pairs%d%d" % (g, u))
-            cast_pairs(nc.scalar.copy, pairs, raw[g, u, 0], 0, 0, HALF)
-            cast_pairs(nc.vector.tensor_copy, pairs, raw[g, u, 1], HALF, 0, vector_share)
-            cast_pairs(nc.scalar.copy, pairs, raw[g, u, 1], HALF, vector_share, HALF)
-            return pairs
 
         def quantise(woven, width, name):
             codes = keep.tile([P, width], U32, name="codes" + name, align_bytes=64)
@@ -120,7 +124,7 @@ def tile_picked_tokscale_none_l_kernel(tc, xT, tscale, cscale, w1_words, w1_scal
                     acc[s, m] = psum.tile([P, SLICE], F32, name="acc%d%d" % (s, m), tag="bank%d" % bank)
                 nc.tensor.matmul_mx(
                     out=acc[s, m][:],
-                    lhsT=w_words[:, g, 2 * P * m : 2 * P * (m + 1)].bitcast(FP4X4),
+                    lhsT=w_words[g][:, 2 * P * m : 2 * P * (m + 1)].bitcast(FP4X4),
                     lhsT_scale=w_scales[:, g, P * m : P * (m + 1)],
                     rhs=codes.bitcast(FP8X4),
                     rhs_scale=scales,
@@ -128,34 +132,55 @@ def tile_picked_tokscale_none_l_kernel(tc, xT, tscale, cscale, w1_words, w1_scal
                     stop=(g == PASSES - 1),
                 )
 
-        picked = [keep.tile([P, 2, S], U32, name="picked%d" % g) for g in range(PASSES)]
-        pairs = make_pairs(0, 0, VECTOR_SHARE)
-        nc.vector.tensor_copy(picked[0][:, 0, :], pairs[:].indirect(offsets[:]))
-        pairs = make_pairs(0, 1, VECTOR_SHARE)
-        halves = [(0, S // 2), (S // 2, S)]
-        for lo, hi in halves:
-            nc.vector.tensor_copy(picked[0][:, 1, lo:hi], pairs[:].indirect(entries(offsets, lo, hi)))
-        woven = {}
-        for lo, hi in halves:
-            woven[lo] = keep.tile([P, 2 * (hi - lo)], U32, name="woven0_%d" % lo, align_bytes=64)
-            weave(nc.vector.tensor_copy, woven[lo][:].bitcast(I32), picked[0][:, :, lo:hi].bitcast(I32))
-        for lo, hi in halves:
-            codes, scales = quantise(woven[lo][:], hi - lo, "0_%d" % lo)
-            for first in range(lo, hi, SLICE):
-                cols = slice(first - lo, first - lo + SLICE)
-                multiply(0, first // SLICE, codes[:, cols], scales[:, cols])
+        PART = S // 2
+        picked0 = [keep.tile([P, 2, PART], U32, name="picked0_%d" % i)[:] for i in range(2)]
+        woven0 = {}
 
-        pairs = make_pairs(1, 0, VECTOR_SHARE_THIRD)
-        nc.vector.tensor_copy(picked[1][:, 0, :], pairs[:].indirect(offsets[:]))
-        pairs = make_pairs(1, 1, VECTOR_SHARE)
+        def gather_parts(u):
+            for i in range(2):
+                nc.vector.tensor_copy(picked0[i][:, u, :], window(u).indirect(entries(offsets, PART * i, PART * (i + 1))))
+
+        def finish_part(i):
+            codes, scales = quantise(woven0[i], PART, "0_%d" % i)
+            for lo in range(0, PART, SLICE):
+                multiply(0, (PART * i + lo) // SLICE, codes[:, lo : lo + SLICE], scales[:, lo : lo + SLICE])
+
+        open_window(0)
+        cast(nc.vector.tensor_copy, 0, 0, 0, HALF)
+        cast_shared(0)
+        gather_parts(0)
+        t_cols = open_window(1, SLICES)
+        nc.scalar.copy(out=t_cols, in_=turned[:, :, P - 1])
+        spread = psum.tile([P, SLICES, P], F32, name="spread", tag="bank1")
+        for s in range(SLICES):
+            nc.tensor.transpose(spread[:, s, :], t_cols[:, s : s + 1].to_broadcast([P, P]), ident[:])
+        cast(nc.scalar.copy, 1, 0, 0, HALF)
+        cast_shared(1)
+        gather_parts(1)
+        for i in range(2):
+            woven0[i] = keep.tile([P, 2 * PART], U32, name="woven0_%d" % i, align_bytes=64)[:]
+            weave(nc.vector.tensor_copy, woven0[i].bitcast(I32), picked0[i].bitcast(I32))
+        for i in range(2):
+            finish_part(i)
+
+        picked1 = keep.tile([P, 2, S], U32, name="picked1")
+        t_picked = open_window(2, S)
+        nc.scalar.copy(out=t_picked, in_=spread[:].rearrange("q s p -> q (s p)"))
+        cast(nc.scalar.copy, 2, 0, 0, HALF)
+        cast_shared(2, VECTOR_SHARE_THIRD)
+        open_window(3)
+        nc.vector.tensor_copy(picked1[:, 0, :], window(2).indirect(offsets[:]))
+        cast(nc.scalar.copy, 3, 0, 0, HALF)
+        cast_shared(3)
 
         starts = range(0, S, SLICE)
+        woven1 = {}
         for lo in starts:
-            nc.vector.tensor_copy(picked[1][:, 1, lo : lo + SLICE], pairs[:].indirect(entries(offsets, lo, lo + SLICE)))
-            woven[lo] = keep.tile([P, 2 * SLICE], U32, name="woven1_%d" % lo, align_bytes=64)
-            weave(nc.scalar.copy, woven[lo][:], picked[1][:, :, lo : lo + SLICE])
+            nc.vector.tensor_copy(picked1[:, 1, lo : lo + SLICE], window(3).indirect(entries(offsets, lo, lo + SLICE)))
+            woven1[lo] = keep.tile([P, 2 * SLICE], U32, name="woven1_%d" % lo, align_bytes=64)
+            weave(nc.scalar.copy, woven1[lo][:], picked1[:, :, lo : lo + SLICE])
         for lo in starts:
-            codes, scales = quantise(woven[lo][:], SLICE, "1_%d" % lo)
+            codes, scales = quantise(woven1[lo][:], SLICE, "1_%d" % lo)
             multiply(1, lo // SLICE, codes[:], scales[:])
 
         queues = (nc.sync, nc.scalar)

@@ -15,6 +15,7 @@ U8 = mybir.dt.uint8
 FP8X4 = mybir.dt.float8_e4m3fn_x4
 FP4X4 = mybir.dt.float4_e2m1fn_x4
 MULT = mybir.AluOpType.mult
+ADD = mybir.AluOpType.add
 
 P = 128
 K_PASS = 4 * P
@@ -27,7 +28,7 @@ M_TILES = N // P
 BANKS = SLICES * M_TILES
 LINE = 4
 VECTOR_SHARE = 352
-VECTOR_SHARE_THIRD = 160
+GPSIMD_SHARE = 256
 
 
 def cast_pairs(copy, pairs, rows):
@@ -55,12 +56,11 @@ def tile_picked_tokscale_none_l_kernel(tc, xT, tscale, cscale, w1_words, w1_scal
         psum = ctx.enter_context(tc.psum_pool(name="psum", bufs=1))
 
         offsets = keep.tile([P, S // PER_COLUMN], U16, name="offsets")
-        nc.sync.dma_start(offsets[:], offs)
         t_row = keep.tile([P, T], F32, name="t_row")
         nc.scalar.dma_start(out=t_row[P - 1 : P, :], in_=tscale[0:1, :])
         nc.vector.memset(t_row[0 : P - 1, :], 0.0)
 
-        w_words = [keep.tile([P, 2 * N], U8, name="w_words%d" % g, align_bytes=64) for g in range(PASSES)]
+        w_words = keep.tile([P, PASSES, 2 * N], U8, name="w_words", align_bytes=64)
         w_scales = keep.tile([P, PASSES, N], U8, name="w_scales", align_bytes=64)
         nc.gpsimd.memset(w_scales[:].bitcast(I32), 0)
 
@@ -72,14 +72,14 @@ def tile_picked_tokscale_none_l_kernel(tc, xT, tscale, cscale, w1_words, w1_scal
             for h in range(2):
                 raw[n, h] = keep.tile([P, 2, HALF], F32, name="raw%d%d" % (n, h), tag="raw%d%d" % (n, h), align_bytes=64)
                 nc.sync.dma_start(out=raw[n, h][:], in_=rows[:, 2 * u : 2 * u + 2, first[n, h] : first[n, h] + HALF])
-                if (n, h) == (2, 1):
-                    for q in range(4):
-                        nc.sync.dma_start(
-                            out=w_scales[32 * q : 32 * q + 4, :, :].bitcast(I32),
-                            in_=w1_scales[:, 4 * q : 4 * q + 4, :].rearrange("g r n -> r g n").bitcast(I32),
-                        )
-                    nc.sync.dma_start(out=w_words[0][:].bitcast(I32), in_=w1_words[0].bitcast(I32))
-        nc.sync.dma_start(out=w_words[1][:].bitcast(I32), in_=w1_words[1].bitcast(I32))
+                if (n, h) == (0, 0):
+                    nc.sync.dma_start(offsets[:], offs)
+        nc.sync.dma_start(out=w_words[:].bitcast(I32), in_=w1_words.rearrange("g p n -> p g n").bitcast(I32))
+        for q in range(4):
+            nc.sync.dma_start(
+                out=w_scales[32 * q : 32 * q + 4, :, :].bitcast(I32),
+                in_=w1_scales[:, 4 * q : 4 * q + 4, :].rearrange("g r n -> r g n").bitcast(I32),
+            )
         c_cols = keep.tile([P, M_TILES], F32, name="c_cols")
         with nc.allow_non_contiguous_dma(reason="one channel scale for each partition"):
             nc.sync.dma_start(out=c_cols[:], in_=cscale.rearrange("(m p) o -> p (m o)", p=P))
@@ -99,9 +99,20 @@ def tile_picked_tokscale_none_l_kernel(tc, xT, tscale, cscale, w1_words, w1_scal
         def cast(copy, n, h, lo, hi):
             cast_pairs(copy, window(n)[:, first[n, h] + lo : first[n, h] + hi], raw[n, h][:, :, lo:hi])
 
-        def cast_shared(n, share=VECTOR_SHARE):
-            cast(nc.vector.tensor_copy, n, 1, 0, share)
-            cast(nc.scalar.copy, n, 1, share, HALF)
+        def cast_first(n):
+            nc.gpsimd.tensor_scalar(
+                out=window(n)[:, 0:GPSIMD_SHARE].bitcast(BF16).rearrange("p (c e) -> p c e", e=2),
+                in0=raw[n, 0][:, :, 0:GPSIMD_SHARE].rearrange("p e c -> p c e"),
+                scalar1=1.0,
+                scalar2=0.0,
+                op0=MULT,
+                op1=ADD,
+            )
+            cast(nc.scalar.copy, n, 0, GPSIMD_SHARE, HALF)
+
+        def cast_shared(n):
+            cast(nc.vector.tensor_copy, n, 1, 0, VECTOR_SHARE)
+            cast(nc.scalar.copy, n, 1, VECTOR_SHARE, HALF)
 
         t_last = keep.tile([P, S], F32, name="t_last")
         nc.vector.tensor_copy(t_last[:], t_row[:].indirect(offsets[:]))
@@ -124,7 +135,7 @@ def tile_picked_tokscale_none_l_kernel(tc, xT, tscale, cscale, w1_words, w1_scal
                     acc[s, m] = psum.tile([P, SLICE], F32, name="acc%d%d" % (s, m), tag="bank%d" % bank)
                 nc.tensor.matmul_mx(
                     out=acc[s, m][:],
-                    lhsT=w_words[g][:, 2 * P * m : 2 * P * (m + 1)].bitcast(FP4X4),
+                    lhsT=w_words[:, g, 2 * P * m : 2 * P * (m + 1)].bitcast(FP4X4),
                     lhsT_scale=w_scales[:, g, P * m : P * (m + 1)],
                     rhs=codes.bitcast(FP8X4),
                     rhs_scale=scales,
@@ -146,7 +157,7 @@ def tile_picked_tokscale_none_l_kernel(tc, xT, tscale, cscale, w1_words, w1_scal
                 multiply(0, (PART * i + lo) // SLICE, codes[:, lo : lo + SLICE], scales[:, lo : lo + SLICE])
 
         open_window(0)
-        cast(nc.vector.tensor_copy, 0, 0, 0, HALF)
+        cast(nc.scalar.copy, 0, 0, 0, HALF)
         cast_shared(0)
         gather_parts(0)
         t_cols = open_window(1, SLICES)
@@ -154,23 +165,24 @@ def tile_picked_tokscale_none_l_kernel(tc, xT, tscale, cscale, w1_words, w1_scal
         spread = psum.tile([P, SLICES, P], F32, name="spread", tag="bank1")
         for s in range(SLICES):
             nc.tensor.transpose(spread[:, s, :], t_cols[:, s : s + 1].to_broadcast([P, P]), ident[:])
-        cast(nc.scalar.copy, 1, 0, 0, HALF)
+        cast_first(1)
         cast_shared(1)
         gather_parts(1)
-        for i in range(2):
-            woven0[i] = keep.tile([P, 2 * PART], U32, name="woven0_%d" % i, align_bytes=64)[:]
-            weave(nc.vector.tensor_copy, woven0[i].bitcast(I32), picked0[i].bitcast(I32))
-        for i in range(2):
-            finish_part(i)
+        woven0[0] = keep.tile([P, 2 * PART], U32, name="woven0", align_bytes=64)[:]
+        weave(nc.scalar.copy, woven0[0], picked0[0])
+        finish_part(0)
 
         picked1 = keep.tile([P, 2, S], U32, name="picked1")
         t_picked = open_window(2, S)
         nc.scalar.copy(out=t_picked, in_=spread[:].rearrange("q s p -> q (s p)"))
-        cast(nc.scalar.copy, 2, 0, 0, HALF)
-        cast_shared(2, VECTOR_SHARE_THIRD)
+        cast_first(2)
+        cast_shared(2)
         open_window(3)
+        woven0[1] = window(3)[:, HALF:T]
+        weave(nc.scalar.copy, woven0[1], picked0[1])
         nc.vector.tensor_copy(picked1[:, 0, :], window(2).indirect(offsets[:]))
-        cast(nc.scalar.copy, 3, 0, 0, HALF)
+        finish_part(1)
+        cast_first(3)
         cast_shared(3)
 
         starts = range(0, S, SLICE)

@@ -15,7 +15,6 @@ U8 = mybir.dt.uint8
 FP8X4 = mybir.dt.float8_e4m3fn_x4
 FP4X4 = mybir.dt.float4_e2m1fn_x4
 MULT = mybir.AluOpType.mult
-ADD = mybir.AluOpType.add
 
 P = 128
 K_PASS = 4 * P
@@ -27,8 +26,10 @@ SLICES = S // SLICE
 M_TILES = N // P
 BANKS = SLICES * M_TILES
 LINE = 4
+PART = S // 2
+COPY = mybir.ActivationFunctionType.Copy
+ADD = mybir.AluOpType.add
 VECTOR_SHARE = 352
-GPSIMD_SHARE = 256
 
 
 def cast_pairs(copy, pairs, rows):
@@ -56,30 +57,37 @@ def tile_picked_tokscale_none_l_kernel(tc, xT, tscale, cscale, w1_words, w1_scal
         psum = ctx.enter_context(tc.psum_pool(name="psum", bufs=1))
 
         offsets = keep.tile([P, S // PER_COLUMN], U16, name="offsets")
+        nc.sync.dma_start(offsets[:], offs)
         t_row = keep.tile([P, T], F32, name="t_row")
-        nc.scalar.dma_start(out=t_row[P - 1 : P, :], in_=tscale[0:1, :])
+        nc.sync.dma_start(out=t_row[P - 1 : P, :], in_=tscale[0:1, :])
         nc.vector.memset(t_row[0 : P - 1, :], 0.0)
-
-        w_words = keep.tile([P, PASSES, 2 * N], U8, name="w_words", align_bytes=64)
+        w_words = [keep.tile([P, 2 * N], U8, name="w_words%d" % g, align_bytes=64) for g in range(PASSES)]
         w_scales = keep.tile([P, PASSES, N], U8, name="w_scales", align_bytes=64)
         nc.gpsimd.memset(w_scales[:].bitcast(I32), 0)
 
-        first = {(n, h): HALF * h for n in range(4) for h in range(2)}
+        rows = [xT[K_PASS * g : K_PASS * (g + 1), :].rearrange("(p t) c -> p t c", t=4) for g in range(PASSES)]
         raw = {}
-        for n in range(4):
+        for n in range(2):
             g, u = divmod(n, 2)
-            rows = xT[K_PASS * g : K_PASS * (g + 1), :].rearrange("(p t) c -> p t c", t=4)
             for h in range(2):
                 raw[n, h] = keep.tile([P, 2, HALF], F32, name="raw%d%d" % (n, h), tag="raw%d%d" % (n, h), align_bytes=64)
-                nc.sync.dma_start(out=raw[n, h][:], in_=rows[:, 2 * u : 2 * u + 2, first[n, h] : first[n, h] + HALF])
-                if (n, h) == (0, 0):
-                    nc.sync.dma_start(offsets[:], offs)
-        nc.sync.dma_start(out=w_words[:].bitcast(I32), in_=w1_words.rearrange("g p n -> p g n").bitcast(I32))
+                nc.sync.dma_start(out=raw[n, h][:], in_=rows[g][:, 2 * u : 2 * u + 2, HALF * h : HALF * (h + 1)])
+        row = {}
+        for t in (0, 2, 1, 3):
+            if t == 0:
+                row[t] = [keep.tile([P, HALF], F32, name="row%d_%d" % (t, h), tag="row%d_%d" % (t, h), align_bytes=64) for h in range(2)]
+                for h in range(2):
+                    nc.sync.dma_start(out=row[t][h][:], in_=rows[1][:, t, HALF * h : HALF * (h + 1)])
+                continue
+            row[t] = keep.tile([P, T], F32, name="row%d" % t)
+            nc.sync.dma_start(out=row[t][:], in_=rows[1][:, t, :])
         for q in range(4):
             nc.sync.dma_start(
                 out=w_scales[32 * q : 32 * q + 4, :, :].bitcast(I32),
                 in_=w1_scales[:, 4 * q : 4 * q + 4, :].rearrange("g r n -> r g n").bitcast(I32),
             )
+        for g in range(PASSES):
+            nc.sync.dma_start(out=w_words[g][:].bitcast(I32), in_=w1_words[g].bitcast(I32))
         c_cols = keep.tile([P, M_TILES], F32, name="c_cols")
         with nc.allow_non_contiguous_dma(reason="one channel scale for each partition"):
             nc.sync.dma_start(out=c_cols[:], in_=cscale.rearrange("(m p) o -> p (m o)", p=P))
@@ -97,18 +105,10 @@ def tile_picked_tokscale_none_l_kernel(tc, xT, tscale, cscale, w1_words, w1_scal
             return windows[n][:, 0:T]
 
         def cast(copy, n, h, lo, hi):
-            cast_pairs(copy, window(n)[:, first[n, h] + lo : first[n, h] + hi], raw[n, h][:, :, lo:hi])
+            cast_pairs(copy, window(n)[:, HALF * h + lo : HALF * h + hi], raw[n, h][:, :, lo:hi])
 
-        def cast_first(n):
-            nc.gpsimd.tensor_scalar(
-                out=window(n)[:, 0:GPSIMD_SHARE].bitcast(BF16).rearrange("p (c e) -> p c e", e=2),
-                in0=raw[n, 0][:, :, 0:GPSIMD_SHARE].rearrange("p e c -> p c e"),
-                scalar1=1.0,
-                scalar2=0.0,
-                op0=MULT,
-                op1=ADD,
-            )
-            cast(nc.scalar.copy, n, 0, GPSIMD_SHARE, HALF)
+        def gpsimd_round(dst, src):
+            nc.gpsimd.tensor_scalar(out=dst, in0=src, scalar1=1.0, scalar2=0.0, op0=MULT, op1=ADD)
 
         def cast_shared(n):
             cast(nc.vector.tensor_copy, n, 1, 0, VECTOR_SHARE)
@@ -132,10 +132,10 @@ def tile_picked_tokscale_none_l_kernel(tc, xT, tscale, cscale, w1_words, w1_scal
             for m in range(M_TILES):
                 if g == 0:
                     bank = BANKS - 1 - (M_TILES * s + m)
-                    acc[s, m] = psum.tile([P, SLICE], F32, name="acc%d%d" % (s, m), tag="bank%d" % bank)
+                    acc[s, m] = psum.tile([P, SLICE], F32, name="acc%d%d" % (s, m), tag="bank%d" % bank)[:]
                 nc.tensor.matmul_mx(
-                    out=acc[s, m][:],
-                    lhsT=w_words[:, g, 2 * P * m : 2 * P * (m + 1)].bitcast(FP4X4),
+                    out=acc[s, m],
+                    lhsT=w_words[g][:, 2 * P * m : 2 * P * (m + 1)].bitcast(FP4X4),
                     lhsT_scale=w_scales[:, g, P * m : P * (m + 1)],
                     rhs=codes.bitcast(FP8X4),
                     rhs_scale=scales,
@@ -143,16 +143,16 @@ def tile_picked_tokscale_none_l_kernel(tc, xT, tscale, cscale, w1_words, w1_scal
                     stop=(g == PASSES - 1),
                 )
 
-        PART = S // 2
-        picked0 = [keep.tile([P, 2, PART], U32, name="picked0_%d" % i)[:] for i in range(2)]
-        woven0 = {}
+        lower = keep.tile([P, PART, 2], U32, name="woven_lower", align_bytes=64)
+        upper = keep.tile([P, 2, PART], U32, name="picked_upper")
+        picked0 = [lower[:].rearrange("p j u -> p u j"), upper[:]]
 
         def gather_parts(u):
-            for i in range(2):
+            for i in (1, 0):
                 nc.vector.tensor_copy(picked0[i][:, u, :], window(u).indirect(entries(offsets, PART * i, PART * (i + 1))))
 
-        def finish_part(i):
-            codes, scales = quantise(woven0[i], PART, "0_%d" % i)
+        def finish_part(i, woven):
+            codes, scales = quantise(woven, PART, "0_%d" % i)
             for lo in range(0, PART, SLICE):
                 multiply(0, (PART * i + lo) // SLICE, codes[:, lo : lo + SLICE], scales[:, lo : lo + SLICE])
 
@@ -165,35 +165,48 @@ def tile_picked_tokscale_none_l_kernel(tc, xT, tscale, cscale, w1_words, w1_scal
         spread = psum.tile([P, SLICES, P], F32, name="spread", tag="bank1")
         for s in range(SLICES):
             nc.tensor.transpose(spread[:, s, :], t_cols[:, s : s + 1].to_broadcast([P, P]), ident[:])
-        cast_first(1)
+        cast(nc.scalar.copy, 1, 0, 0, HALF)
         cast_shared(1)
         gather_parts(1)
-        woven0[0] = keep.tile([P, 2 * PART], U32, name="woven0", align_bytes=64)[:]
-        weave(nc.scalar.copy, woven0[0], picked0[0])
-        finish_part(0)
-
-        picked1 = keep.tile([P, 2, S], U32, name="picked1")
-        t_picked = open_window(2, S)
+        after = keep.tile([P, S + 2 * PART], U32, name="after", tag="raw11", align_bytes=64)
+        t_picked = after[:, 0:S].bitcast(F32)
         nc.scalar.copy(out=t_picked, in_=spread[:].rearrange("q s p -> q (s p)"))
-        cast_first(2)
-        cast_shared(2)
-        open_window(3)
-        woven0[1] = window(3)[:, HALF:T]
+        woven0 = [lower[:].rearrange("p j u -> p (j u)"), after[:, S:]]
         weave(nc.scalar.copy, woven0[1], picked0[1])
-        nc.vector.tensor_copy(picked1[:, 0, :], window(2).indirect(offsets[:]))
-        finish_part(1)
-        cast_first(3)
-        cast_shared(3)
 
-        starts = range(0, S, SLICE)
-        woven1 = {}
-        for lo in starts:
-            nc.vector.tensor_copy(picked1[:, 1, lo : lo + SLICE], window(3).indirect(entries(offsets, lo, lo + SLICE)))
-            woven1[lo] = keep.tile([P, 2 * SLICE], U32, name="woven1_%d" % lo, align_bytes=64)
-            weave(nc.scalar.copy, woven1[lo][:], picked1[:, :, lo : lo + SLICE])
-        for lo in starts:
-            codes, scales = quantise(woven1[lo][:], SLICE, "1_%d" % lo)
-            multiply(1, lo // SLICE, codes[:], scales[:])
+        for i in range(2):
+            finish_part(i, woven0[i])
+        woven1 = []
+
+        def open_slices(words):
+            for i in range(2):
+                woven1.append(words[:, PART * i : PART * (i + 1)].bitcast(BF16).rearrange("p (j t) -> p j t", t=4))
+
+        for i in range(2):
+            open_slices(woven0[i])
+
+        def slice_entries(s):
+            return entries(offsets, s * SLICE, (s + 1) * SLICE)
+
+        rounded = [keep.tile([P, T], BF16, name="rounded%d" % t)[:] for t in range(2)]
+        for s in range(SLICES):
+            nc.vector.tensor_copy(woven1[s][:, :, 2], row[2][:].indirect(slice_entries(s)))
+        for h in range(2):
+            gpsimd_round(rounded[0][:, HALF * h : HALF * (h + 1)], row[0][h][:])
+        gpsimd_round(rounded[1], row[1][:])
+        for t in range(2):
+            for s in range(SLICES):
+                nc.scalar.activation(woven1[s][:, :, t], rounded[t].indirect(slice_entries(s)), COPY)
+
+        def finish_slice(s):
+            codes, scales = quantise(woven1[s].rearrange("p j t -> p (j t)"), SLICE, "1_%d" % s)
+            multiply(1, s, codes[:], scales[:])
+
+        for s in range(SLICES):
+            nc.vector.tensor_copy(woven1[s][:, :, 3], row[3][:].indirect(slice_entries(s)))
+            if s:
+                finish_slice(s - 1)
+        finish_slice(SLICES - 1)
 
         queues = (nc.sync, nc.scalar)
         out_tiles = out.rearrange("(m p) j -> p m j", p=P)
@@ -204,7 +217,7 @@ def tile_picked_tokscale_none_l_kernel(tc, xT, tscale, cscale, w1_words, w1_scal
             for m in range(M_TILES):
                 nc.vector.scalar_tensor_tensor(
                     out=result[:, m, :],
-                    in0=acc[s, m][:],
+                    in0=acc[s, m],
                     scalar=c_cols[:, m : m + 1],
                     in1=t_picked[:, cols],
                     op0=MULT,

@@ -29,21 +29,7 @@ LINE = 4
 PART = S // 2
 COPY = mybir.ActivationFunctionType.Copy
 ADD = mybir.AluOpType.add
-VECTOR_SHARE = 352
-
-
-def cast_pairs(copy, pairs, rows):
-    copy(
-        out=pairs.bitcast(BF16).rearrange("p (c i e) -> p c e i", i=LINE, e=2),
-        in_=rows.rearrange("p e (c i) -> p c e i", i=LINE),
-    )
-
-
-def weave(copy, woven, picked):
-    copy(
-        out=woven.rearrange("p (c i u) -> p c u i", i=LINE, u=2),
-        in_=picked.rearrange("p u (c i) -> p c u i", i=LINE),
-    )
+LOAD_ORDER = (0, 2, 1, 3)
 
 
 def entries(offsets, lo, hi):
@@ -59,28 +45,19 @@ def tile_picked_tokscale_none_l_kernel(tc, xT, tscale, cscale, w1_words, w1_scal
         offsets = keep.tile([P, S // PER_COLUMN], U16, name="offsets")
         nc.sync.dma_start(offsets[:], offs)
         t_row = keep.tile([P, T], F32, name="t_row")
-        nc.sync.dma_start(out=t_row[P - 1 : P, :], in_=tscale[0:1, :])
+        nc.scalar.dma_start(out=t_row[P - 1 : P, :], in_=tscale[0:1, :])
         nc.vector.memset(t_row[0 : P - 1, :], 0.0)
         w_words = [keep.tile([P, 2 * N], U8, name="w_words%d" % g, align_bytes=64) for g in range(PASSES)]
         w_scales = keep.tile([P, PASSES, N], U8, name="w_scales", align_bytes=64)
         nc.gpsimd.memset(w_scales[:].bitcast(I32), 0)
 
-        rows = [xT[K_PASS * g : K_PASS * (g + 1), :].rearrange("(p t) c -> p t c", t=4) for g in range(PASSES)]
-        raw = {}
-        for n in range(2):
-            g, u = divmod(n, 2)
-            for h in range(2):
-                raw[n, h] = keep.tile([P, 2, HALF], F32, name="raw%d%d" % (n, h), tag="raw%d%d" % (n, h), align_bytes=64)
-                nc.sync.dma_start(out=raw[n, h][:], in_=rows[g][:, 2 * u : 2 * u + 2, HALF * h : HALF * (h + 1)])
         row = {}
-        for t in (0, 2, 1, 3):
-            if t == 0:
-                row[t] = [keep.tile([P, HALF], F32, name="row%d_%d" % (t, h), tag="row%d_%d" % (t, h), align_bytes=64) for h in range(2)]
-                for h in range(2):
-                    nc.sync.dma_start(out=row[t][h][:], in_=rows[1][:, t, HALF * h : HALF * (h + 1)])
-                continue
-            row[t] = keep.tile([P, T], F32, name="row%d" % t)
-            nc.sync.dma_start(out=row[t][:], in_=rows[1][:, t, :])
+        for g in range(PASSES):
+            rows = xT[K_PASS * g : K_PASS * (g + 1), :].rearrange("(p t) c -> p t c", t=4)
+            for t in LOAD_ORDER:
+                name = "row%d%d" % (g, t)
+                row[g, t] = keep.tile([P, T], F32, name=name, tag=name, align_bytes=64)
+                nc.sync.dma_start(out=row[g, t][:], in_=rows[:, t, :])
         for q in range(4):
             nc.sync.dma_start(
                 out=w_scales[32 * q : 32 * q + 4, :, :].bitcast(I32),
@@ -94,26 +71,6 @@ def tile_picked_tokscale_none_l_kernel(tc, xT, tscale, cscale, w1_words, w1_scal
         ident = keep.tile([P, P], F32, name="ident")
         make_identity(nc, ident[:])
 
-        windows = {}
-
-        def open_window(n, spare=0):
-            tag = "raw%d1" % (n - 1) if n else "window0"
-            windows[n] = keep.tile([P, T + spare], U32, name="window%d" % n, tag=tag, align_bytes=64)
-            return windows[n][:, T : T + spare].bitcast(F32) if spare else None
-
-        def window(n):
-            return windows[n][:, 0:T]
-
-        def cast(copy, n, h, lo, hi):
-            cast_pairs(copy, window(n)[:, HALF * h + lo : HALF * h + hi], raw[n, h][:, :, lo:hi])
-
-        def gpsimd_round(dst, src):
-            nc.gpsimd.tensor_scalar(out=dst, in0=src, scalar1=1.0, scalar2=0.0, op0=MULT, op1=ADD)
-
-        def cast_shared(n):
-            cast(nc.vector.tensor_copy, n, 1, 0, VECTOR_SHARE)
-            cast(nc.scalar.copy, n, 1, VECTOR_SHARE, HALF)
-
         t_last = keep.tile([P, S], F32, name="t_last")
         nc.vector.tensor_copy(t_last[:], t_row[:].indirect(offsets[:]))
         turned = psum.tile([P, SLICES, P], F32, name="turned", tag="bank0")
@@ -123,7 +80,7 @@ def tile_picked_tokscale_none_l_kernel(tc, xT, tscale, cscale, w1_words, w1_scal
         def quantise(woven, width, name):
             codes = keep.tile([P, width], U32, name="codes" + name, align_bytes=64)
             scales = keep.tile([P, width], U8, name="scales" + name, align_bytes=64)
-            nc.vector.quantize_mx(out=codes[:].bitcast(FP8X4), scales=scales[:], in_=woven.bitcast(BF16))
+            nc.vector.quantize_mx(out=codes[:].bitcast(FP8X4), scales=scales[:], in_=woven.rearrange("p j t -> p (j t)"))
             return codes, scales
 
         acc = {}
@@ -143,67 +100,50 @@ def tile_picked_tokscale_none_l_kernel(tc, xT, tscale, cscale, w1_words, w1_scal
                     stop=(g == PASSES - 1),
                 )
 
-        lower = keep.tile([P, PART, 2], U32, name="woven_lower", align_bytes=64)
-        upper = keep.tile([P, 2, PART], U32, name="picked_upper")
-        picked0 = [lower[:].rearrange("p j u -> p u j"), upper[:]]
+        def round_row(g, t, tag=None):
+            rounded = keep.tile([P, T], BF16, name="rounded%d%d" % (g, t), tag=tag or "rounded%d%d" % (g, t), align_bytes=64)
+            nc.gpsimd.tensor_scalar(out=rounded[:], in0=row[g, t][:], scalar1=1.0, scalar2=0.0, op0=MULT, op1=ADD)
+            return rounded
 
-        def gather_parts(u):
-            for i in (1, 0):
-                nc.vector.tensor_copy(picked0[i][:, u, :], window(u).indirect(entries(offsets, PART * i, PART * (i + 1))))
+        def scalar_gather(woven, t, rounded, lo, hi):
+            nc.scalar.activation(woven[:, lo:hi, t], rounded[:].indirect(entries(offsets, lo, hi)), COPY)
 
-        def finish_part(i, woven):
-            codes, scales = quantise(woven, PART, "0_%d" % i)
-            for lo in range(0, PART, SLICE):
-                multiply(0, (PART * i + lo) // SLICE, codes[:, lo : lo + SLICE], scales[:, lo : lo + SLICE])
+        def vector_gather(woven, g, t, lo, hi):
+            nc.vector.tensor_copy(woven[:, lo:hi, t], row[g, t][:].indirect(entries(offsets, lo, hi)))
 
-        open_window(0)
-        cast(nc.scalar.copy, 0, 0, 0, HALF)
-        cast_shared(0)
-        gather_parts(0)
-        t_cols = open_window(1, SLICES)
-        nc.scalar.copy(out=t_cols, in_=turned[:, :, P - 1])
+        woven0 = keep.tile([P, S, 4], BF16, name="woven0", align_bytes=64)
+        scalar_gather(woven0, 0, round_row(0, 0), 0, S)
+        vector_gather(woven0, 0, 2, 0, S)
+        t_cols = keep.tile([P, SLICES], F32, name="t_cols")
+        nc.scalar.copy(out=t_cols[:], in_=turned[:, :, P - 1])
         spread = psum.tile([P, SLICES, P], F32, name="spread", tag="bank1")
         for s in range(SLICES):
             nc.tensor.transpose(spread[:, s, :], t_cols[:, s : s + 1].to_broadcast([P, P]), ident[:])
-        cast(nc.scalar.copy, 1, 0, 0, HALF)
-        cast_shared(1)
-        gather_parts(1)
-        after = keep.tile([P, S + 2 * PART], U32, name="after", tag="raw11", align_bytes=64)
-        t_picked = after[:, 0:S].bitcast(F32)
+        rounded = round_row(0, 1)
+        for lo in range(0, S, PART):
+            scalar_gather(woven0, 1, rounded, lo, lo + PART)
+        vector_gather(woven0, 0, 3, 0, S)
+        t_picked = keep.tile([P, S], F32, name="t_picked", tag="rounded01", align_bytes=64)[:]
         nc.scalar.copy(out=t_picked, in_=spread[:].rearrange("q s p -> q (s p)"))
-        woven0 = [lower[:].rearrange("p j u -> p (j u)"), after[:, S:]]
-        weave(nc.scalar.copy, woven0[1], picked0[1])
+        for part in range(0, S, PART):
+            codes, scales = quantise(woven0[:, part : part + PART, :], PART, "0_%d" % part)
+            for lo in range(0, PART, SLICE):
+                multiply(0, (part + lo) // SLICE, codes[:, lo : lo + SLICE], scales[:, lo : lo + SLICE])
 
-        for i in range(2):
-            finish_part(i, woven0[i])
-        woven1 = []
-
-        def open_slices(words):
-            for i in range(2):
-                woven1.append(words[:, PART * i : PART * (i + 1)].bitcast(BF16).rearrange("p (j t) -> p j t", t=4))
-
-        for i in range(2):
-            open_slices(woven0[i])
-
-        def slice_entries(s):
-            return entries(offsets, s * SLICE, (s + 1) * SLICE)
-
-        rounded = [keep.tile([P, T], BF16, name="rounded%d" % t)[:] for t in range(2)]
-        for s in range(SLICES):
-            nc.vector.tensor_copy(woven1[s][:, :, 2], row[2][:].indirect(slice_entries(s)))
-        for h in range(2):
-            gpsimd_round(rounded[0][:, HALF * h : HALF * (h + 1)], row[0][h][:])
-        gpsimd_round(rounded[1], row[1][:])
-        for t in range(2):
-            for s in range(SLICES):
-                nc.scalar.activation(woven1[s][:, :, t], rounded[t].indirect(slice_entries(s)), COPY)
+        woven1 = woven0
+        rounded = [round_row(1, t) for t in range(2)]
+        for lo in range(0, S, PART):
+            scalar_gather(woven1, 0, rounded[0], lo, lo + PART)
+            vector_gather(woven1, 1, 2, lo, lo + PART)
+        for lo in range(0, S, SLICE):
+            scalar_gather(woven1, 1, rounded[1], lo, lo + SLICE)
 
         def finish_slice(s):
-            codes, scales = quantise(woven1[s].rearrange("p j t -> p (j t)"), SLICE, "1_%d" % s)
+            codes, scales = quantise(woven1[:, s * SLICE : (s + 1) * SLICE, :], SLICE, "1_%d" % s)
             multiply(1, s, codes[:], scales[:])
 
         for s in range(SLICES):
-            nc.vector.tensor_copy(woven1[s][:, :, 3], row[3][:].indirect(slice_entries(s)))
+            vector_gather(woven1, 1, 3, s * SLICE, (s + 1) * SLICE)
             if s:
                 finish_slice(s - 1)
         finish_slice(SLICES - 1)

@@ -29,7 +29,7 @@ LINE = 4
 PART = S // 2
 COPY = mybir.ActivationFunctionType.Copy
 ADD = mybir.AluOpType.add
-LOAD_ORDER = (0, 2, 1, 3)
+LOAD_ORDER = (0, 1, 2, 3)
 
 
 def entries(offsets, lo, hi):
@@ -100,53 +100,48 @@ def tile_picked_tokscale_none_l_kernel(tc, xT, tscale, cscale, w1_words, w1_scal
                     stop=(g == PASSES - 1),
                 )
 
-        def round_row(g, t, tag=None):
-            rounded = keep.tile([P, T], BF16, name="rounded%d%d" % (g, t), tag=tag or "rounded%d%d" % (g, t), align_bytes=64)
-            nc.gpsimd.tensor_scalar(out=rounded[:], in0=row[g, t][:], scalar1=1.0, scalar2=0.0, op0=MULT, op1=ADD)
-            return rounded
-
-        def scalar_gather(woven, t, rounded, lo, hi):
-            nc.scalar.activation(woven[:, lo:hi, t], rounded[:].indirect(entries(offsets, lo, hi)), COPY)
-
         def vector_gather(woven, g, t, lo, hi):
             nc.vector.tensor_copy(woven[:, lo:hi, t], row[g, t][:].indirect(entries(offsets, lo, hi)))
 
-        woven0 = keep.tile([P, S, 4], BF16, name="woven0", align_bytes=64)
-        scalar_gather(woven0, 0, round_row(0, 0), 0, S)
-        vector_gather(woven0, 0, 2, 0, S)
+        def scalar_gather(picked, g, t, lo, hi):
+            nc.scalar.activation(picked[:, t % 2, lo - PART : hi - PART], row[g, t][:].indirect(entries(offsets, lo, hi)), COPY)
+
+        def placed(woven, picked, u, lo, hi):
+            return woven[:, lo:hi, 2 * u : 2 * u + 2], picked[:, :, lo:hi].rearrange("p t j -> p j t")
+
+        low = keep.tile([P, PART, 4], BF16, name="low", align_bytes=64)
+        high = keep.tile([P, PART, 4], BF16, name="high", align_bytes=64)
         t_cols = keep.tile([P, SLICES], F32, name="t_cols")
-        nc.scalar.copy(out=t_cols[:], in_=turned[:, :, P - 1])
-        spread = psum.tile([P, SLICES, P], F32, name="spread", tag="bank1")
-        for s in range(SLICES):
-            nc.tensor.transpose(spread[:, s, :], t_cols[:, s : s + 1].to_broadcast([P, P]), ident[:])
-        rounded = round_row(0, 1)
-        for lo in range(0, S, PART):
-            scalar_gather(woven0, 1, rounded, lo, lo + PART)
-        vector_gather(woven0, 0, 3, 0, S)
-        t_picked = keep.tile([P, S], F32, name="t_picked", tag="rounded01", align_bytes=64)[:]
-        nc.scalar.copy(out=t_picked, in_=spread[:].rearrange("q s p -> q (s p)"))
-        for part in range(0, S, PART):
-            codes, scales = quantise(woven0[:, part : part + PART, :], PART, "0_%d" % part)
-            for lo in range(0, PART, SLICE):
-                multiply(0, (part + lo) // SLICE, codes[:, lo : lo + SLICE], scales[:, lo : lo + SLICE])
-
-        woven1 = woven0
-        rounded = [round_row(1, t) for t in range(2)]
-        for lo in range(0, S, PART):
-            scalar_gather(woven1, 0, rounded[0], lo, lo + PART)
-            vector_gather(woven1, 1, 2, lo, lo + PART)
-        for lo in range(0, S, SLICE):
-            scalar_gather(woven1, 1, rounded[1], lo, lo + SLICE)
-
-        def finish_slice(s):
-            codes, scales = quantise(woven1[:, s * SLICE : (s + 1) * SLICE, :], SLICE, "1_%d" % s)
-            multiply(1, s, codes[:], scales[:])
-
-        for s in range(SLICES):
-            vector_gather(woven1, 1, 3, s * SLICE, (s + 1) * SLICE)
-            if s:
-                finish_slice(s - 1)
-        finish_slice(SLICES - 1)
+        t_picked = keep.tile([P, S], F32, name="t_picked", align_bytes=64)[:]
+        for g in range(PASSES):
+            for u in range(2):
+                picked = keep.tile([P, 2, PART], BF16, name="picked%d%d" % (g, u), align_bytes=64)
+                last = g == PASSES - 1 and u == 1
+                for t in (2 * u, 2 * u + 1):
+                    step = SLICE if last and t % 2 else PART
+                    for lo in range(0, PART, step):
+                        vector_gather(low, g, t, lo, lo + step)
+                        scalar_gather(picked, g, t, PART + lo, PART + lo + step)
+                    if g == 0 and t == 0:
+                        nc.scalar.copy(out=t_cols[:], in_=turned[:, :, P - 1])
+                        spread = psum.tile([P, SLICES, P], F32, name="spread", tag="bank1")
+                        for s in range(SLICES):
+                            nc.tensor.transpose(spread[:, s, :], t_cols[:, s : s + 1].to_broadcast([P, P]), ident[:])
+                    if g == 0 and t == 1:
+                        nc.scalar.copy(out=t_picked, in_=spread[:].rearrange("q s p -> q (s p)"))
+                if last:
+                    for lo in range(0, PART, SLICE):
+                        dst, src = placed(high, picked, u, lo, lo + SLICE)
+                        nc.scalar.copy(out=dst, in_=src)
+                else:
+                    dst, src = placed(high, picked, u, 0, PART)
+                    nc.gpsimd.tensor_scalar(out=dst, in0=src, scalar1=1.0, scalar2=0.0, op0=MULT, op1=ADD)
+            width = PART if g == 0 else SLICE
+            for half, woven in enumerate((low, high)):
+                for part in range(0, PART, width):
+                    codes, scales = quantise(woven[:, part : part + width, :], width, "%d_%d_%d" % (g, half, part))
+                    for lo in range(0, width, SLICE):
+                        multiply(g, (half * PART + part + lo) // SLICE, codes[:, lo : lo + SLICE], scales[:, lo : lo + SLICE])
 
         queues = (nc.sync, nc.scalar)
         out_tiles = out.rearrange("(m p) j -> p m j", p=P)

@@ -51,6 +51,12 @@ def tile_picked_tokscale_none_l_kernel(tc, xT, tscale, cscale, w1_words, w1_scal
         w_scales = keep.tile([P, PASSES, N], U8, name="w_scales", align_bytes=64)
         nc.gpsimd.memset(w_scales[:].bitcast(I32), 0)
 
+        for q in range(4):
+            nc.scalar.dma_start(
+                out=w_scales[32 * q : 32 * q + 4, :, :].bitcast(I32),
+                in_=w1_scales[:, 4 * q : 4 * q + 4, :].rearrange("g r n -> r g n").bitcast(I32),
+            )
+
         row = {}
         for g in range(PASSES):
             rows = xT[K_PASS * g : K_PASS * (g + 1), :].rearrange("(p t) c -> p t c", t=4)
@@ -58,13 +64,8 @@ def tile_picked_tokscale_none_l_kernel(tc, xT, tscale, cscale, w1_words, w1_scal
                 name = "row%d%d" % (g, t)
                 row[g, t] = keep.tile([P, T], F32, name=name, tag=name, align_bytes=64)
                 nc.sync.dma_start(out=row[g, t][:], in_=rows[:, t, :])
-        for q in range(4):
-            nc.sync.dma_start(
-                out=w_scales[32 * q : 32 * q + 4, :, :].bitcast(I32),
-                in_=w1_scales[:, 4 * q : 4 * q + 4, :].rearrange("g r n -> r g n").bitcast(I32),
-            )
-        for g in range(PASSES):
-            nc.sync.dma_start(out=w_words[g][:].bitcast(I32), in_=w1_words[g].bitcast(I32))
+                if g == PASSES - 1 and t >= 2:
+                    nc.sync.dma_start(out=w_words[t - 2][:].bitcast(I32), in_=w1_words[t - 2].bitcast(I32))
         c_cols = keep.tile([P, M_TILES], F32, name="c_cols")
         with nc.allow_non_contiguous_dma(reason="one channel scale for each partition"):
             nc.sync.dma_start(out=c_cols[:], in_=cscale.rearrange("(m p) o -> p (m o)", p=P))

@@ -44,7 +44,7 @@ def tile_picked_tokscale_none_l_kernel(tc, xT, tscale, cscale, w1_words, w1_scal
 
         offsets = keep.tile([P, S // PER_COLUMN], U16, name="offsets")
         nc.sync.dma_start(offsets[:], offs)
-        t_row = keep.tile([P, T], F32, name="t_row")
+        t_row = keep.tile([P, T], F32, name="t_row", tag="woven0", align_bytes=64)
         nc.scalar.dma_start(out=t_row[P - 1 : P, :], in_=tscale[0:1, :])
         nc.vector.memset(t_row[0 : P - 1, :], 0.0)
         w_words = [keep.tile([P, 2 * N], U8, name="w_words%d" % g, align_bytes=64) for g in range(PASSES)]
@@ -60,17 +60,26 @@ def tile_picked_tokscale_none_l_kernel(tc, xT, tscale, cscale, w1_words, w1_scal
         row = {}
         for g in range(PASSES):
             rows = xT[K_PASS * g : K_PASS * (g + 1), :].rearrange("(p t) c -> p t c", t=4)
-            for t in LOAD_ORDER:
+            for t in range(4):
                 name = "row%d%d" % (g, t)
-                row[g, t] = keep.tile([P, T], F32, name=name, tag=name, align_bytes=64)
-                nc.sync.dma_start(out=row[g, t][:], in_=rows[:, t, :])
+                if g == 0 and t < 2:
+                    if t == 0:
+                        both = keep.tile([P, 2, T], F32, name=name, align_bytes=64)
+                        nc.sync.dma_start(out=both[:], in_=rows[:, 0:2, :])
+                    row[g, t] = both[:, t, :]
+                    continue
+                row[g, t] = keep.tile([P, T], F32, name=name, tag=name, align_bytes=64)[:]
+                nc.sync.dma_start(out=row[g, t], in_=rows[:, t, :])
                 if g == PASSES - 1 and t >= 2:
                     nc.sync.dma_start(out=w_words[t - 2][:].bitcast(I32), in_=w1_words[t - 2].bitcast(I32))
         c_cols = keep.tile([P, M_TILES], F32, name="c_cols")
         with nc.allow_non_contiguous_dma(reason="one channel scale for each partition"):
             nc.sync.dma_start(out=c_cols[:], in_=cscale.rearrange("(m p) o -> p (m o)", p=P))
         ident = keep.tile([P, P], F32, name="ident")
-        make_identity(nc, ident[:])
+        zero = keep.tile([P, 1], F32, name="zero")
+        nc.gpsimd.memset(zero[:], 0.0)
+        nc.scalar.activation(ident[:], zero[:].to_broadcast([P, P]), COPY)
+        make_identity(nc, ident[:], nomemset=True)
 
         t_last = keep.tile([P, S], F32, name="t_last")
         nc.vector.tensor_copy(t_last[:], t_row[:].indirect(offsets[:]))
@@ -102,21 +111,23 @@ def tile_picked_tokscale_none_l_kernel(tc, xT, tscale, cscale, w1_words, w1_scal
                 )
 
         def vector_gather(woven, g, t, lo, hi):
-            nc.vector.tensor_copy(woven[:, lo:hi, t], row[g, t][:].indirect(entries(offsets, lo, hi)))
+            nc.vector.tensor_copy(woven[:, lo:hi, t], row[g, t].indirect(entries(offsets, lo, hi)))
 
         def scalar_gather(picked, g, t, lo, hi):
-            nc.scalar.activation(picked[:, t % 2, lo - PART : hi - PART], row[g, t][:].indirect(entries(offsets, lo, hi)), COPY)
+            nc.scalar.activation(picked[:, t % 2, lo - PART : hi - PART], row[g, t].indirect(entries(offsets, lo, hi)), COPY)
 
         def placed(woven, picked, u, lo, hi):
             return woven[:, lo:hi, 2 * u : 2 * u + 2], picked[:, :, lo:hi].rearrange("p t j -> p j t")
 
-        low = keep.tile([P, PART, 4], BF16, name="low", align_bytes=64)
-        high = keep.tile([P, PART, 4], BF16, name="high", align_bytes=64)
+        woven0 = keep.tile([P, S, 4], BF16, name="woven0", tag="woven0", align_bytes=64)
+        low1 = keep.tile([P, PART, 4], BF16, name="low1", align_bytes=64)
+        high = woven0[:, PART:, :]
         t_cols = keep.tile([P, SLICES], F32, name="t_cols")
         t_picked = keep.tile([P, S], F32, name="t_picked", align_bytes=64)[:]
         for g in range(PASSES):
+            low = low1[:] if g else woven0[:, :PART, :]
             for u in range(2):
-                picked = keep.tile([P, 2, PART], BF16, name="picked%d%d" % (g, u), align_bytes=64)
+                picked = keep.tile([P, 2, PART], BF16 if g + u else F32, name="picked%d%d" % (g, u), align_bytes=64)
                 last = g == PASSES - 1 and u == 1
                 for t in (2 * u, 2 * u + 1):
                     step = SLICE if last and t % 2 else PART
@@ -137,12 +148,15 @@ def tile_picked_tokscale_none_l_kernel(tc, xT, tscale, cscale, w1_words, w1_scal
                 else:
                     dst, src = placed(high, picked, u, 0, PART)
                     nc.gpsimd.tensor_scalar(out=dst, in0=src, scalar1=1.0, scalar2=0.0, op0=MULT, op1=ADD)
-            width = PART if g == 0 else SLICE
-            for half, woven in enumerate((low, high)):
-                for part in range(0, PART, width):
-                    codes, scales = quantise(woven[:, part : part + width, :], width, "%d_%d_%d" % (g, half, part))
-                    for lo in range(0, width, SLICE):
-                        multiply(g, (half * PART + part + lo) // SLICE, codes[:, lo : lo + SLICE], scales[:, lo : lo + SLICE])
+            if g == 0:
+                codes, scales = quantise(woven0[:], S, "0")
+                for s in range(SLICES):
+                    multiply(0, s, codes[:, s * SLICE : (s + 1) * SLICE], scales[:, s * SLICE : (s + 1) * SLICE])
+                continue
+            for s in range(SLICES):
+                lo = s * SLICE % PART
+                codes, scales = quantise((low, high)[s * SLICE // PART][:, lo : lo + SLICE, :], SLICE, "1_%d" % s)
+                multiply(1, s, codes[:], scales[:])
 
         queues = (nc.sync, nc.scalar)
         out_tiles = out.rearrange("(m p) j -> p m j", p=P)

@@ -40,6 +40,7 @@ def tile_picked_tokscale_none_l_kernel(tc, xT, tscale, cscale, w1_words, w1_scal
     nc = tc.nc
     with ExitStack() as ctx:
         keep = ctx.enter_context(tc.tile_pool(name="keep", bufs=1))
+        shelf = ctx.enter_context(tc.tile_pool(name="shelf", bufs=1))
         psum = ctx.enter_context(tc.psum_pool(name="psum", bufs=1))
 
         offsets = keep.tile([P, S // PER_COLUMN], U16, name="offsets")
@@ -81,7 +82,7 @@ def tile_picked_tokscale_none_l_kernel(tc, xT, tscale, cscale, w1_words, w1_scal
         nc.scalar.activation(ident[:], zero[:].to_broadcast([P, P]), COPY)
         make_identity(nc, ident[:], nomemset=True)
 
-        t_last = keep.tile([P, S], F32, name="t_last")
+        t_last = shelf.tile([P, S], F32, name="t_last", offset=0, align_bytes=64)
         nc.vector.tensor_copy(t_last[:], t_row[:].indirect(offsets[:]))
         turned = psum.tile([P, SLICES, P], F32, name="turned", tag="bank0")
         for s in range(SLICES):
@@ -123,11 +124,14 @@ def tile_picked_tokscale_none_l_kernel(tc, xT, tscale, cscale, w1_words, w1_scal
         low1 = keep.tile([P, PART, 4], BF16, name="low1", align_bytes=64)
         high = woven0[:, PART:, :]
         t_cols = keep.tile([P, SLICES], F32, name="t_cols")
-        t_picked = keep.tile([P, S], F32, name="t_picked", align_bytes=64)[:]
         for g in range(PASSES):
             low = low1[:] if g else woven0[:, :PART, :]
             for u in range(2):
-                picked = keep.tile([P, 2, PART], BF16 if g + u else F32, name="picked%d%d" % (g, u), align_bytes=64)
+                name = "picked%d%d" % (g, u)
+                if g + u == 0:
+                    picked = keep.tile([P, 2, PART], F32, name=name, align_bytes=64)
+                else:
+                    picked = shelf.tile([P, 2, PART], BF16, name=name, offset=1024 * (g + u), align_bytes=64)
                 last = g == PASSES - 1 and u == 1
                 for t in (2 * u, 2 * u + 1):
                     step = SLICE if last and t % 2 else PART
@@ -139,9 +143,13 @@ def tile_picked_tokscale_none_l_kernel(tc, xT, tscale, cscale, w1_words, w1_scal
                         spread = psum.tile([P, SLICES, P], F32, name="spread", tag="bank1")
                         for s in range(SLICES):
                             nc.tensor.transpose(spread[:, s, :], t_cols[:, s : s + 1].to_broadcast([P, P]), ident[:])
-                    if g == 0 and t == 1:
+                    if g == 1 and t == 1:
+                        t_picked = keep.tile([P, S], F32, name="t_picked", tag="row11", align_bytes=64)[:]
                         nc.scalar.copy(out=t_picked, in_=spread[:].rearrange("q s p -> q (s p)"))
-                if last:
+                if g == 0 and u == 1:
+                    dst, src = placed(high, picked, u, 0, PART)
+                    nc.scalar.copy(out=dst, in_=src)
+                elif last:
                     for lo in range(0, PART, SLICE):
                         dst, src = placed(high, picked, u, lo, lo + SLICE)
                         nc.scalar.copy(out=dst, in_=src)

from contextlib import ExitStack

import concourse.mybir as mybir
from concourse.masks import make_identity

K, T, S, N = 1024, 1024, 512, 256
FLOPS = 2 * K * S * N

F32 = mybir.dt.float32
BF16 = mybir.dt.bfloat16
I32 = mybir.dt.int32
U32 = mybir.dt.uint32
U16 = mybir.dt.uint16
U8 = mybir.dt.uint8
FP8X4 = mybir.dt.float8_e4m3fn_x4
FP4X4 = mybir.dt.float4_e2m1fn_x4
MULT = mybir.AluOpType.mult

P = 128
K_PASS = 4 * P
PASSES = K // K_PASS
PER_COLUMN = 16
HALF = T // 2
SLICE = 128
SLICES = S // SLICE
M_TILES = N // P
BANKS = SLICES * M_TILES
LINE = 4
PART = S // 2
COPY = mybir.ActivationFunctionType.Copy
ADD = mybir.AluOpType.add
LOAD_ORDER = (0, 1, 2, 3)


def entries(offsets, lo, hi):
    return offsets[:, lo // PER_COLUMN : hi // PER_COLUMN]


def tile_picked_tokscale_none_l_kernel(tc, xT, tscale, cscale, w1_words, w1_scales, offs, out):
    nc = tc.nc
    with ExitStack() as ctx:
        keep = ctx.enter_context(tc.tile_pool(name="keep", bufs=1))
        shelf = ctx.enter_context(tc.tile_pool(name="shelf", bufs=1))
        psum = ctx.enter_context(tc.psum_pool(name="psum", bufs=1))

        offsets = keep.tile([P, S // PER_COLUMN], U16, name="offsets")
        nc.sync.dma_start(offsets[:], offs)
        t_row = keep.tile([P, T], F32, name="t_row", tag="woven0", align_bytes=64)
        nc.scalar.dma_start(out=t_row[P - 1 : P, :], in_=tscale[0:1, :])
        nc.vector.memset(t_row[0 : P - 1, :], 0.0)
        w_words = [keep.tile([P, 2 * N], U8, name="w_words%d" % g, align_bytes=64) for g in range(PASSES)]
        w_scales = keep.tile([P, PASSES, N], U8, name="w_scales", align_bytes=64)
        nc.gpsimd.memset(w_scales[:].bitcast(I32), 0)

        for q in range(4):
            nc.scalar.dma_start(
                out=w_scales[32 * q : 32 * q + 4, :, :].bitcast(I32),
                in_=w1_scales[:, 4 * q : 4 * q + 4, :].rearrange("g r n -> r g n").bitcast(I32),
            )

        row = {}
        for g in range(PASSES):
            rows = xT[K_PASS * g : K_PASS * (g + 1), :].rearrange("(p t) c -> p t c", t=4)
            for t in range(4):
                name = "row%d%d" % (g, t)
                if g == 0 and t < 2:
                    if t == 0:
                        both = keep.tile([P, 2, T], F32, name=name, align_bytes=64)
                        nc.sync.dma_start(out=both[:], in_=rows[:, 0:2, :])
                    row[g, t] = both[:, t, :]
                    continue
                row[g, t] = keep.tile([P, T], F32, name=name, tag=name, align_bytes=64)[:]
                nc.sync.dma_start(out=row[g, t], in_=rows[:, t, :])
                if g == PASSES - 1 and t >= 2:
                    nc.sync.dma_start(out=w_words[t - 2][:].bitcast(I32), in_=w1_words[t - 2].bitcast(I32))
        c_cols = keep.tile([P, M_TILES], F32, name="c_cols")
        with nc.allow_non_contiguous_dma(reason="one channel scale for each partition"):
            nc.sync.dma_start(out=c_cols[:], in_=cscale.rearrange("(m p) o -> p (m o)", p=P))
        ident = keep.tile([P, P], F32, name="ident")
        zero = keep.tile([P, 1], F32, name="zero")
        nc.gpsimd.memset(zero[:], 0.0)
        nc.scalar.activation(ident[:], zero[:].to_broadcast([P, P]), COPY)
        make_identity(nc, ident[:], nomemset=True)

        t_last = shelf.tile([P, S], F32, name="t_last", offset=0, align_bytes=64)
        nc.vector.tensor_copy(t_last[:], t_row[:].indirect(offsets[:]))
        turned = psum.tile([P, SLICES, P], F32, name="turned", tag="bank0")
        for s in range(SLICES):
            nc.tensor.transpose(turned[:, s, :], t_last[:, s * P : (s + 1) * P], ident[:])

        def quantise(woven, width, name):
            codes = keep.tile([P, width], U32, name="codes" + name, align_bytes=64)
            scales = keep.tile([P, width], U8, name="scales" + name, align_bytes=64)
            nc.vector.quantize_mx(out=codes[:].bitcast(FP8X4), scales=scales[:], in_=woven.rearrange("p j t -> p (j t)"))
            return codes, scales

        acc = {}

        def multiply(g, s, codes, scales):
            for m in range(M_TILES):
                if g == 0:
                    bank = BANKS - 1 - (M_TILES * s + m)
                    acc[s, m] = psum.tile([P, SLICE], F32, name="acc%d%d" % (s, m), tag="bank%d" % bank)[:]
                nc.tensor.matmul_mx(
                    out=acc[s, m],
                    lhsT=w_words[g][:, 2 * P * m : 2 * P * (m + 1)].bitcast(FP4X4),
                    lhsT_scale=w_scales[:, g, P * m : P * (m + 1)],
                    rhs=codes.bitcast(FP8X4),
                    rhs_scale=scales,
                    start=(g == 0),
                    stop=(g == PASSES - 1),
                )

        def vector_gather(woven, g, t, lo, hi):
            nc.vector.tensor_copy(woven[:, lo:hi, t], row[g, t].indirect(entries(offsets, lo, hi)))

        def scalar_gather(picked, g, t, lo, hi):
            nc.scalar.activation(picked[:, t % 2, lo - PART : hi - PART], row[g, t].indirect(entries(offsets, lo, hi)), COPY)

        def placed(woven, picked, u, lo, hi):
            return woven[:, lo:hi, 2 * u : 2 * u + 2], picked[:, :, lo:hi].rearrange("p t j -> p j t")

        woven0 = keep.tile([P, S, 4], BF16, name="woven0", tag="woven0", align_bytes=64)
        low1 = keep.tile([P, PART, 4], BF16, name="low1", align_bytes=64)
        high = woven0[:, PART:, :]
        t_cols = keep.tile([P, SLICES], F32, name="t_cols")
        for g in range(PASSES):
            low = low1[:] if g else woven0[:, :PART, :]
            for u in range(2):
                name = "picked%d%d" % (g, u)
                if g + u == 0:
                    picked = keep.tile([P, 2, PART], F32, name=name, align_bytes=64)
                else:
                    picked = shelf.tile([P, 2, PART], BF16, name=name, offset=1024 * (g + u), align_bytes=64)
                last = g == PASSES - 1 and u == 1
                for t in (2 * u, 2 * u + 1):
                    step = SLICE if last and t % 2 else PART
                    for lo in range(0, PART, step):
                        vector_gather(low, g, t, lo, lo + step)
                        scalar_gather(picked, g, t, PART + lo, PART + lo + step)
                    if g == 0 and t == 0:
                        nc.scalar.copy(out=t_cols[:], in_=turned[:, :, P - 1])
                        spread = psum.tile([P, SLICES, P], F32, name="spread", tag="bank1")
                        for s in range(SLICES):
                            nc.tensor.transpose(spread[:, s, :], t_cols[:, s : s + 1].to_broadcast([P, P]), ident[:])
                    if g == 1 and t == 1:
                        t_picked = keep.tile([P, S], F32, name="t_picked", tag="row11", align_bytes=64)[:]
                        nc.scalar.copy(out=t_picked, in_=spread[:].rearrange("q s p -> q (s p)"))
                if g == 0 and u == 1:
                    dst, src = placed(high, picked, u, 0, PART)
                    nc.scalar.copy(out=dst, in_=src)
                elif last:
                    for lo in range(0, PART, SLICE):
                        dst, src = placed(high, picked, u, lo, lo + SLICE)
                        nc.scalar.copy(out=dst, in_=src)
                else:
                    dst, src = placed(high, picked, u, 0, PART)
                    nc.gpsimd.tensor_scalar(out=dst, in0=src, scalar1=1.0, scalar2=0.0, op0=MULT, op1=ADD)
            if g == 0:
                codes, scales = quantise(woven0[:], S, "0")
                for s in range(SLICES):
                    multiply(0, s, codes[:, s * SLICE : (s + 1) * SLICE], scales[:, s * SLICE : (s + 1) * SLICE])
                continue
            for s in range(SLICES):
                lo = s * SLICE % PART
                codes, scales = quantise((low, high)[s * SLICE // PART][:, lo : lo + SLICE, :], SLICE, "1_%d" % s)
                multiply(1, s, codes[:], scales[:])

        queues = (nc.sync, nc.scalar)
        out_tiles = out.rearrange("(m p) j -> p m j", p=P)
        for s in range(SLICES):
            cols = slice(s * SLICE, (s + 1) * SLICE)
            last = s == SLICES - 1
            result = keep.tile([P, M_TILES, SLICE], F32, name="result%d" % s)
            for m in range(M_TILES):
                nc.vector.scalar_tensor_tensor(
                    out=result[:, m, :],
                    in0=acc[s, m],
                    scalar=c_cols[:, m : m + 1],
                    in1=t_picked[:, cols],
                    op0=MULT,
                    op1=MULT,
                )
                if last:
                    queues[(s + m) % 2].dma_start(out=out_tiles[:, m, cols], in_=result[:, m, :])
            if not last:
                queues[s % 2].dma_start(out=out_tiles[:, :, cols], in_=result[:])
